import numpy as np, ml_dtypes
CORES = [3,11,19,27,35,43,51,59]
N = 8
BF = ml_dtypes.bfloat16
W, L, S, T, F = 4096, 256, 2, 4, 128
C = W >> S
LEVELS = np.array([800, 900, 1000, 1050, 1100, 1150, 1250, 1400])
def parts(rng):
    d = {"key": rng.integers(0, 256, (N, 8, 16, W)), "em": rng.integers(0, 256, (N, 8, 16, W)), "cl": rng.integers(0, W, (N, 8, 16, C)), "pl": rng.integers(0, W, (N, 8, 16, L)),
         "q": rng.integers(0, 256, (N, 8, 16, L)), "emb": rng.integers(0, 256, (N, 8, 16, 16)), "w": rng.integers(0, 256, (N, 8, 16, 1))}
    base = np.stack([rng.permutation(LEVELS) for r in range(N)]).reshape(N, 8, 1, 1)
    d["th"] = base + rng.integers(-100, 101, (N, 8, 16, 1))
    return d
def pack(d):
    kinds = {"key": BF, "em": BF, "cl": np.int32, "pl": np.int32, "q": BF, "emb": BF, "w": BF, "th": np.float32}
    return {k: np.ascontiguousarray(d[k].reshape(N, 128, -1)).astype(np.float32).astype(t) for k, t in kinds.items()}
def setup_inputs(rng):
    return pack(parts(rng))
def setup_inputs_ties(rng):
    d = parts(rng); o = rng.permutation(8)
    for k in ("key", "q", "emb"): d[k] = 64 * rng.integers(0, 4, d[k].shape)
    d["th"] = 64 * rng.integers(16, 23, (N, 8, 16, 1)) + rng.integers(0, 2, (N, 8, 16, 1))
    d["em"] = rng.integers(0, 2, (N, 8, 16, W)) * rng.choice(np.array([1, 3, 255]), (N, 8, 1, 1))
    d["em"][:, o[0]] = 7; d["em"][:, o[1]] = 0
    for k in ("key", "q", "emb"):
        d[k][:, o[2]] = 0
        d[k][:, o[3]] = rng.integers(0, 32, d[k][:, o[3]].shape)
    d["th"][:, o[2], :, 0] = rng.permutation(np.arange(16) % 3)
    d["th"][:, o[3]] = rng.integers(1, 256, (N, 16, 1))
    return pack(d)
def setup_inputs_ends(rng):
    d = parts(rng); o = rng.permutation(8); ends = np.array([0, 1, W - 2, W - 1])
    d["pl"][:, o[0]] = rng.choice(ends, (N, 16, L)); d["th"][:, o[0]] = 4096
    d["th"][:, o[1]] = 0
    d["pl"][:, o[2]] = rng.integers(0, W, (N, 1, L))
    d["cl"][:, o[3]] = rng.choice(ends, (N, 16, C)); d["th"][:, o[3]] = 1000
    d["cl"][:, o[4]] = rng.integers(0, W, (N, 1, C))
    d["key"][:, o[5]] = d["key"][:, o[5]][:, :, :1]
    d["pl"][:, o[6]] = rng.choice(ends, (N, 16, L))
    d["th"][:, o[7]] = 0; d["w"][:, o[7]] = 0
    return pack(d)
def setup_inputs_lone(rng):
    d = parts(rng); d["th"] = np.zeros((N, 8, 16, 1), np.int64)
    for r in range(N):
        o = rng.permutation(8)
        d["th"][r, o[1], 0] = 4096; d["th"][r, o[2], 15] = 4096; d["th"][r, o[3], 14:] = 4096
        for g in o[4:]: d["th"][r, g, rng.integers(1, 15)] = 4096
    d["th"][rng.integers(0, N)] = 0
    return pack(d)
def setup_inputs_big(rng):
    d = parts(rng); o = rng.permutation(8)
    for k in ("key", "em", "q", "emb"): d[k] = 255 * rng.integers(0, 2, d[k].shape)
    d["w"] = rng.integers(254, 256, d["w"].shape)
    d["th"] = rng.choice(np.array([1785, 1786, 2040, 2041, 2295, 1020, 4080, 4081]), (N, 8, 16, 1))
    d["key"][:, o[0]] = 0; d["q"][:, o[0]] = 255; d["emb"][:, o[0]] = 255; d["w"][:, o[0]] = 255
    d["th"][:, o[0], :, 0] = 4080 + np.arange(16) % 2
    d["em"][:, o[1]] = 255
    d["th"][:, o[2]] = 0
    d["th"][:, o[3]] = 0; d["q"][:, o[3]] = 255; d["emb"][:, o[3]] = 255; d["w"][:, o[3]] = 255
    d["em"][:, o[4]] = 255 - (rng.random((N, 16, W)) < 0.0625)
    return pack(d)
def setup_inputs_spread(rng):
    d = parts(rng)
    for k in ("key", "em", "q", "emb"):
        s = d[k].shape
        d[k] = np.minimum((np.exp2(10 * rng.random(s[:2] + (1, s[3]))) * rng.random(s)).astype(np.int64), 255)
    d["w"] = np.minimum(np.exp2(8 * rng.random(d["w"].shape)).astype(np.int64), 255)
    d["th"] = np.minimum(np.exp2(8 + 4 * rng.random((N, 8, 16, 1))).astype(np.int64), 4096)
    for k in ("pl", "cl"): d[k] = np.minimum((W * rng.random(d[k].shape) ** 3).astype(np.int64), W - 1)
    return pack(d)
def check_inputs(d):
    bad = []
    for k, hi in (("key", 255), ("em", 255), ("cl", W - 1), ("pl", W - 1), ("q", 255), ("emb", 255), ("w", 255), ("th", 4096)):
        a = np.asarray(d[k]).astype(np.float64)
        if not np.all((a >= 0) & (a <= hi) & (a == np.floor(a))): bad.append("whole numbers and range of " + k)
    return bad
def reference(key, em, cl, pl, q, emb, w, th):
    def ints(a): return a.astype(np.float32).astype(np.int32).reshape(N, 8, 16, -1)
    K, E, CL, B, H, TH = ints(key), ints(em), ints(cl), ints(emb), ints(w), ints(th)
    p, x = ints(pl), ints(q)
    toks = [[] for r in range(N)]
    for t in range(T):
        pn, xn = [], []
        for r in range(N):
            at = np.take_along_axis(K[r], p[r].reshape(8, 1, 16 * L), 2).reshape(8, 16, 16, L)
            dist = np.add.reduce(np.abs(at - x[r][:, :, None, :]), axis=1)
            near = dist < TH[r]
            first = np.argmax(near, axis=1)
            lead = np.take_along_axis(p[r], first[:, None, :], 1)[:, 0]
            h = np.add.reduce(H[r] * x[r], axis=1)
            c = np.where(np.any(near, axis=1), lead >> S, h & (C - 1))
            pr = np.where(near, p[r], np.take_along_axis(CL[r], c[:, None, :], 2))
            v = np.add.reduce(np.take_along_axis(E[r], pr.reshape(8, 1, 16 * L), 2).reshape(8, 16, 16, L), axis=2)
            tok = np.argmax(v, axis=1)
            toks[r].append(tok)
            xn.append((x[r] + np.take_along_axis(B[r], tok[:, :, None], 1).transpose(0, 2, 1)) >> 1); pn.append(pr)
        p = np.stack([np.concatenate([(pn[(r - 1) % N][..., :F] + (1 if r == 0 else 0)) & (W - 1), (pn[(r + 1) % N][..., F:] - (1 if r == N - 1 else 0)) & (W - 1)], axis=2) for r in range(N)])
        x = np.stack([np.concatenate([xn[(r - 1) % N][..., :F], xn[(r + 1) % N][..., F:]], axis=2) for r in range(N)])
    yt = np.stack([np.concatenate(a, axis=1) for a in toks])
    return {"yp": p.reshape(N, 128, L).astype(np.float32), "yq": x.reshape(N, 128, L).astype(np.float32).astype(BF), "yt": yt.astype(np.float32)}

@@ -1,0 +1,403 @@
+from concourse.mybir import dt, AluOpType, AxisListType, ActivationFunctionType
+
+A = AluOpType
+CH = ("F", "B")
+STEPS = 4
+BIG = 12582912.0
+PL = {"cyc": 0.83, "pe": 0.45, "ga": 1.6, "hop": 110.0, "pipe": 70.0, "rem": 3600.0, "load": 3000.0, "chunk": 32,
+      "s": 0.0, "x": 0.0, "e": 450.0, "k": 600.0, "n": 100.0, "lag": 0.0, "ve": 0.0, "vk": 300.0}
+
+SCRATCH = {}
+SEMAPHORES = ["vs", "ss", "ts", "gs", "lsent", "oyt"]
+BF, HF, F32, I32, U16 = "bfloat16", "float16", "float32", "int32", "uint16"
+
+
+def _sb(dtype, cols, names, suffix=""):
+    for nm in names.split():
+        SCRATCH[nm + suffix] = ("sbuf", [128, cols], dtype)
+
+
+_sb(BF, 4096, "s_key s_em")
+_sb(I32, 1024, "s_cl")
+_sb(I32, 256, "s_pl")
+_sb(BF, 256, "s_q")
+_sb(BF, 16, "s_emb s_w BD8 TK")
+_sb(F32, 8, "s_th BDF KC")
+SEMAPHORES += ["l" + k for k in SCRATCH if k[0] == "s"]
+_sb(BF, 128, "ONE IB T1 BD LT VB0 VBT I16 IHF NBD LTM WA WX CA XC QC DEB MASK")
+_sb(HF, 128, "IH IH4 BDH")
+_sb(BF, 144, "BM1 B2")
+_sb(F32, 128, "RST")
+_sb(I32, 128, "MI MJ")
+_sb(I32, 8, "COI")
+_sb(U16, 16, "CO")
+_sb(F32, 1024, "CLT YT")
+_sb(F32, 256, "YP")
+for _x in CH:
+    _sb(BF, 2048, "K MX E", _x)
+    _sb(U16, 128, "P0 PW", _x)
+    _sb(HF, 128, "PF R NP NQ Z M", _x)
+    _sb(BF, 128, "NE NN U UT", _x)
+    _sb(U16, 16, "COF", _x)
+    _sb(F32, 128, "ST PM SC", _x)
+    _sb(I32, 128, "W1 W2", _x)
+    for _t in range(STEPS):
+        _sb(U16, 128, "PS", "%s%d" % (_x, _t))
+        _sb(BF, 128, "QS", "%s%d" % (_x, _t))
+        _sb(U16, 128, "LP", "%s%d" % (_x, _t + 1))
+        _sb(BF, 128, "LQ", "%s%d" % (_x, _t + 1))
+        SEMAPHORES += ["ap%s%d" % (_x, _t + 1), "aq%s%d" % (_x, _t + 1)]
+    SEMAPHORES += ["oy" + _x, "oq" + _x]
+for _k in range(8):
+    SCRATCH["b%d" % _k] = ("psum", [128, 512], F32)
+SIZE = {BF: 2, HF: 2, U16: 2, F32: 4, I32: 4}
+
+
+def rank_program(g, core, T, topo):
+    rank = T.rank_of(core)
+    if rank is None:
+        return
+    n = len(T.cores)
+    Q = {"v": g.vector, "s": g.scalar, "t": g.tensor, "g": g, "y": g.sync}
+    OWN = {"v": "vs", "s": "ss", "t": "ts", "g": "gs"}
+    cnt = {"vs": 0, "ss": 0, "ts": 0, "gs": 0, "lsent": 0}
+    clk = {q: 0.0 for q in Q}
+    know = {q: {} for q in Q}
+    acc = {}
+    bank = {}
+    seq = [0]
+
+    def need(q, toks):
+        kn = know[q]
+        for o, sem, val, snap, tm, oq in sorted(toks, key=lambda a: -a[0]):
+            if kn.get(sem, 0) >= val:
+                continue
+            Q[q].wait_ge(T.sem[sem], val)
+            for s, v in snap.items():
+                if kn.get(s, 0) < v:
+                    kn[s] = v
+            kn[sem] = val
+
+    def deps(q, reads, writes):
+        toks = []
+        for regs, wr in ((reads, False), (writes, True)):
+            for name, lo, hi in regs:
+                if name[0] == "b":
+                    for oq, (lw, la) in bank.get(name, {}).items():
+                        if oq != q:
+                            toks.append(la)
+                        elif q != "t" and not wr and lw is not None:
+                            toks.append(lw)
+                    continue
+                for e in acc.get(name, []):
+                    if e[0] < hi and lo < e[1] and (e[2] or wr):
+                        if e[3] == q and not e[2]:
+                            continue
+                        toks.append(e[4])
+        return toks
+
+    def start_of(d):
+        q, dur, fn, reads, writes = d[:5]
+        t0 = clk[q]
+        for k in deps(q, reads, writes):
+            t0 = max(t0, k[4] + (PL["pipe"] if k[5] == q else PL["hop"]))
+        return t0
+
+    def emit(d, quiet=False):
+        q, dur, fn, reads, writes, sem, inc = d
+        t0 = start_of(d)
+        if quiet:
+            t0, dur = max(k[4] for k in deps(q, reads, writes)), 0.0
+        need(q, deps(q, reads, writes))
+        ins = fn(Q[q])
+        seq[0] += 1
+        end = t0 + dur
+        if not quiet:
+            clk[q] = end
+        if ins is None:
+            return
+        if sem is None:
+            sem = OWN[q]
+            cnt[sem] += 1
+            val = cnt[sem]
+        else:
+            val = inc
+            end += PL["load"]
+        ins.then_inc(T.sem[sem], inc)
+        note(q, (seq[0], sem, val, dict(know[q]), end, q), reads, writes)
+
+    def note(q, tok, reads, writes):
+        for regs, wr in ((writes, True), (reads, False)):
+            for name, lo, hi in regs:
+                if name[0] == "b":
+                    d = bank.setdefault(name, {})
+                    lw = d[q][0] if q in d else None
+                    d[q] = (tok if wr else lw, tok)
+                    continue
+                l = acc.setdefault(name, [])
+                if wr:
+                    l[:] = [e for e in l if not (lo <= e[0] and e[1] <= hi)]
+                l.append((lo, hi, wr, q, tok))
+
+    def op(q, dur, fn, reads, writes, sem=None, inc=1):
+        return (q, dur, fn, reads, writes, sem, inc)
+
+    def ap(r):
+        return T[r[0]][:, r[1]:r[2]]
+
+    def R(name, lo=0, hi=None):
+        return (name, lo, SCRATCH[name][1][1] if hi is None else hi)
+
+    def vcost(regs, n, two=False):
+        c = 2.0 if two else 0.5 if all(SIZE[SCRATCH[r[0]][2]] == 2 for r in regs) else 1.0
+        return max(64.0, n * c) * PL["cyc"]
+
+    def ts(out, in0, s1, s2, op0, op1=None, extra=(), oap=None, iap=None):
+        a, b = (ap(out) if oap is None else oap), (ap(in0) if iap is None else iap)
+        dur = vcost((out, in0), out[2] - out[1] if oap is None else 8)
+        if op1 is None:
+            return op("v", dur, lambda e: e.tensor_scalar(a, b, s1, None, op0), [in0] + list(extra), [out])
+        return op("v", dur, lambda e: e.tensor_scalar(a, b, s1, s2, op0, op1), [in0] + list(extra), [out])
+
+    def tt(out, in0, in1, o, extra=(), iap=None, ind=False):
+        b = ap(in0) if iap is None else iap
+        m = out[2] - out[1]
+        dur = 50 + m * PL["ga"] * PL["cyc"] if ind else vcost((out, in0, in1), m, in0[0][0] != "b" and in1[0][0] != "b")
+        return op("v", dur, lambda e: e.tensor_tensor(ap(out), b, ap(in1), o), [in0, in1] + list(extra), [out])
+
+    def vcopy(out, in_, iap=None):
+        b = ap(in_) if iap is None else iap
+        return op("v", vcost((out, in_), out[2] - out[1]), lambda e: e.tensor_copy(ap(out), b), [in_], [out])
+
+    def fill(reg, c, fap=None):
+        a = ap(reg) if fap is None else fap
+        return op("v", vcost((reg,), reg[2]), lambda e: e.memset(a, c), [], [reg])
+
+    def mm(out, lhs, rhs, start, stop, rap=None, oap=None):
+        a, b = (ap(out) if oap is None else oap), (ap(rhs) if rap is None else rap)
+        return op("t", max(64, out[2] - out[1]) * PL["pe"], lambda e: e.matmul(a, ap(lhs), b, start, stop), [lhs, rhs], [out])
+
+    def sel(base, a):
+        return R(base, 15 - a, 15 - a + 128)
+
+    for nm in "pl key q w th emb cl em".split():
+        src, d = T[nm][:], "s_" + nm
+        emit(op("y", 60, lambda e: e.dma_start(T[d][:, 0:T[nm].shape[1]], src), [], [R(d)], "l" + d, 16))
+
+    def aff(out, in_, pattern, cmp, base, cm):
+        emit(op("g", 400, lambda e: e.affine_select(ap(R(out)), ap(R(in_)), pattern, cmp, 0.0, base, cm), [R(in_)], [R(out)]))
+    emit(fill(R("ONE"), 1.0))
+    aff("T1", "ONE", [[-16, 8], [0, 16]], A.is_ge, 0, 1)
+    aff("BD", "T1", [[16, 8], [0, 16]], A.is_ge, 15, -1)
+    aff("IB", "ONE", [[-1, 128]], A.is_equal, 0, 1)
+    emit(op("g", 340, lambda e: e.iota(T.VB0[:, :], [[0, 8], [-1, 16]], 15, 0, allow_small_or_imprecise_dtypes=True), [], [R("VB0")]))
+    emit(op("g", 150, lambda e: e.iota(T.COI[:, :], [[16, 8]], 15, 0), [], [R("COI")]))
+    emit(op("g", 340, lambda e: e.iota(T.MI[:, :], [[0, 8], [-1, 16]], 128, 1), [], [R("MI")]))
+    aff("LT", "BD", [[1, 128]], A.is_gt, 0, -1)
+    for b in ("BM1", "B2", "WA", "WX"):
+        emit(fill(R(b), 0.0))
+    for d in (fill(R("CA"), -2.0 ** -7, T.CA[0:64, :]), fill(R("XC"), 32.0), fill(R("QC"), -2.0 ** -9), fill(R("RST"), 1.0),
+              fill(R("CA"), 2.0 ** -17, T.CA[64:128, :]), fill(R("XC"), 64.0, T.XC[:, 15:128:16]), fill(R("RST"), 0.0, T.RST[:, 0:128:16])):
+        emit(d)
+    emit(vcopy(R("BD8", 0, 8), R("BD"), T.BD[:, 0:128:16]))
+    emit(vcopy(R("BDF"), R("BD"), T.BD[:, 0:128:16]))
+    emit(ts(R("NBD"), R("BD"), -1.0, None, A.mult))
+    emit(ts(R("BM1"), R("BD8", 0, 8), -1.0, None, A.mult, oap=T.BM1[:, 15:128:16]))
+    emit(ts(R("B2"), R("BD8", 0, 8), 2.0, None, A.mult, oap=T.B2[:, 15:128:16]))
+    emit(vcopy(R("BDH"), R("BD")))
+    for i, x in enumerate(CH):
+        emit(vcopy(R("P0" + x), R("s_pl", 128 * i, 128 * i + 128)))
+    emit(vcopy(R("IH"), R("IB")))
+    emit(ts(R("IH4"), R("IB"), 4096.0, None, A.mult))
+    emit(ts(R("I16"), R("IB"), 16.0, None, A.mult))
+    emit(ts(R("IHF"), R("IB"), 0.5, None, A.mult))
+    emit(vcopy(R("CO", 0, 8), R("COI")))
+    emit(ts(R("VBT"), R("VB0"), 1.0 / 128, None, A.mult))
+    emit(ts(R("MJ"), R("MI"), 15, None, A.bitwise_and))
+    emit(ts(R("MASK"), R("MJ"), 0.0, -8192.0, A.not_equal, A.mult))
+    emit(ts(R("LTM"), R("LT"), -4096.0, None, A.mult))
+    emit(op("v", 110, lambda e: e.tensor_reduce(T.KC[:, 0:1], T.LT[:, :], AxisListType.X, A.add), [R("LT")], [R("KC")]))
+    emit(ts(R("TK", 0, 8), R("BD8", 0, 8), T.KC[:, 0:1], None, A.mult, extra=[R("KC")]))
+    for q in clk:
+        clk[q] = 0.0
+
+    BK = {"F": ("b0", "b1", "b2", "b6"), "B": ("b3", "b4", "b5", "b7")}
+    threads = []
+    state = {"F": -1, "B": -1}
+    once = {}
+
+    def P(x, t):
+        return R("P0" + x) if t == 0 else R("LP%s%d" % (x, t))
+
+    def QQ(x, t):
+        i = CH.index(x)
+        return R("s_q", 128 * i, 128 * i + 128) if t == 0 else R("LQ%s%d" % (x, t))
+
+    def closing(x):
+        return 1 if (x == "F" and rank == 0) else -1 if (x == "B" and rank == n - 1) else 0
+
+    def gather(out, win, off, c0, c1):
+        w = R(win)
+        o, f = (out, 16 * c0, 16 * c1), (off[0], c0, c1)
+        src = ap(w).indirect(ap(f))
+        d = 16 * (c1 - c0) * PL["ga"] * PL["cyc"]
+        return ([op("s", 65 + d, lambda e: e.activation(ap(o), src, ActivationFunctionType.Copy), [w, f], [o])],
+                [op("v", 50 + d, lambda e: e.tensor_copy(ap(o), src), [w, f], [o])])
+
+    def send(x, t, src, land, sem):
+        dst = T.cores[(rank + 1) % n if x == "F" else (rank - 1) % n]
+        frm = T.cores[(rank - 1) % n if x == "F" else (rank + 1) % n]
+        rid, pid, _ = topo.addr(dst)
+        name = "%s%s%d" % (src, x, t)
+        to, rs = "%s%s%d" % (land, x, t + 1), "%s%s%d" % (sem, x, t + 1)
+
+        def go(e):
+            t0 = start_of(d)
+            e.remote_dma(T[to][:], T[name][:], T.sem[rs], T.sem.lsent, pid, rid, topo.mask(core, dst))
+            cnt["lsent"] += len(topo.engines(core, dst))
+            seq[0] += 1
+            note("r", (seq[0], rs, len(topo.engines(frm, core)), {}, t0 + PL["rem"], "r"), [], [R(to)])
+        d = op("g", 600, go, [R(name)], [])
+        return d
+
+    def moved(x, src, quiet):
+        emit(ts(R("W1" + x), src, float(closing(x)), None, A.add), quiet)
+        emit(ts(R("W2" + x), R("W1" + x), 4095, None, A.bitwise_and), quiet)
+
+    def keys(x, t):
+        p = src = P(x, t)
+        if closing(x) and t:
+            p = R("PW" + x)
+
+        def first(e):
+            if p != src:
+                moved(x, src, True)
+                emit(vcopy(p, R("W2" + x)), True)
+                need("v", deps("v", [p], []))
+            return e.tensor_scalar(ap(R("PF" + x)), ap(p), -1.0, 8193.5, A.mult, A.add)
+        yield "n", [op("v", vcost((p,), 128), first, [src], [R("PF" + x)])]
+        yield "n", [ts(R(BK[x][0], 128, 256), p, -2048.0, None, A.add)]
+        for c in range(0, 128, PL["chunk"]):
+            yield "k", gather("K" + x, "s_key", p, c, c + PL["chunk"])
+        for j in range(0, 16, 4):
+            yield "n", [mm(R(BK[x][1], 0, 128), sel("BM1", i), R("K" + x), i == 0, False, rap=T["K" + x][:, i:2048:16]) for i in range(j, j + 4)]
+        state[x] = t
+
+    def main(x, t):
+        b1, b2, b3, by = BK[x]
+        q = QQ(x, t)
+        one = R("ONE")
+        while state[x] < t:
+            yield None
+        if "w" not in once:
+            once["w"] = 1
+            for b, c in (("WA", 1.0 / 1024), ("WX", -4.0)):
+                yield "s", [ts(R(b), R("BD8", 0, 8), T.s_w[:, 0:1], c, A.mult, A.mult, extra=[R("s_w")], oap=T[b][:, 15:128:16])]
+        yield "s", [mm(R(b1, 0, 128), R("IB"), q, True, True), mm(R(b2, 0, 128), R("NBD"), q, False, False),
+                    mm(R(b3, 128, 256), R("WA"), q, True, False), mm(R(b3, 128, 256), R("CA"), one, False, True)]
+        for i in range(16):
+            o = R("MX" + x, 128 * i, 128 * i + 128)
+            yield "x", [tt(o, R("K" + x), R(b1, 0, 128), A.max, iap=T["K" + x][:, i:2048:16]), mm(R(b2, 0, 128), sel("B2", i), o, False, i == 15)]
+            if i == 5:
+                l = [ts(R("R" + x), R(b3, 128, 256), BIG, -BIG, A.add, A.add)]
+                for o, last in ((R(b3, 0, 128), True), (R(b3, 128, 256), False)):
+                    l += [mm(o, R("WX"), q, True, False), mm(o, R("XC"), one, False, False), mm(o, R("IH4"), R("R" + x), False, last)]
+                yield "x", l
+            if i == 12:
+                yield "x", [tt(R(b1, 256, 384), R("PF" + x), R(b3, 0, 128), A.subtract)]
+        d, xx, cc = R(b2, 0, 128), R(b3, 128, 256), R(b1, 384, 512)
+        th = T.s_th[:, 0:1]
+        ne, nn = R("NE" + x), R("NN" + x)
+        yield "s", [ts(ne, d, th, None, A.is_lt, extra=[R("s_th")]), mm(xx, R("LTM"), ne, False, False)]
+        yield "s", [tt(R("NP" + x), ne, R(b1, 256, 384), A.mult), mm(xx, R("IH"), R("NP" + x), False, True)]
+        yield "s", [ts(nn, d, th, None, A.is_ge, extra=[R("s_th")])]
+        yield "s", [tt(R("NQ" + x), ne, R(b1, 128, 256), A.mult), mm(cc, R("IB"), R("MASK"), True, False), mm(R(b2, 128, 256), R("IH"), R("NQ" + x), True, False)]
+        if "c" not in once:
+            once["c"] = 1
+            yield "s", [ts(R("CLT"), R("s_cl"), -2048.0, None, A.add)]
+        yield "s", [ts(R("Z" + x), xx, -4096.0, 0.0, A.add, A.max), mm(cc, R("BDH"), R("Z" + x), False, True)]
+        sc = R("SC" + x)
+        yield "s", [op("v", 107, lambda e: e.tensor_tensor_scan(ap(sc), ap(R("RST")), ap(cc), 0.0, A.mult, A.max), [R("RST"), cc], [sc])]
+        yield "s", [ts(R("COF" + x, 0, 8), sc, -0.25, 1024.0, A.mult, A.add, iap=T["SC" + x][:, 15:128:16])]
+        w, f = R("CLT"), R("COF" + x, 0, 8)
+        yield "s", [tt(R("M" + x), w, nn, A.mult, extra=[f], iap=ap(w).indirect(ap(f)), ind=True), mm(R(b2, 128, 256), R("IH"), R("M" + x), False, True)]
+        ps = R("PS%s%d" % (x, t))
+        yield "s", [ts(ps, R(b2, 128, 256), 2048.0, None, A.add), send(x, t, "PS", "LP", "ap")]
+        if t + 1 < STEPS:
+            threads.append([x, keys(x, t + 1), None])
+        for c in range(0, 128, PL["chunk"]):
+            yield "e", gather("E" + x, "s_em", ps, c, c + PL["chunk"])
+        for c0 in (0, 64):
+            o = R(b3, 256 + c0, 320 + c0)
+            yield "s", [mm(o, R("VBT"), R("ONE", 0, 64), True, False)] + [
+                mm(o, R("I16"), ("E" + x, 16 * c0, 16 * c0 + 1024), False, i == 15, rap=T["E" + x][:, 16 * c0 + i:16 * c0 + 1024:16]) for i in range(16)]
+        st, pm, u, ut, co = R("ST" + x), R("PM" + x), R("U" + x), R("UT" + x), R("CO", 0, 8)
+        if "e" not in once:
+            once["e"] = 1
+            for j in range(8):
+                yield "s", [ts(R("DEB", 16 * j, 16 * j + 16), R("s_emb"), T.BDF[:, j:j + 1], 0.5, A.mult, A.mult, extra=[R("BDF")])]
+        yield "s", [op("v", 107, lambda e: e.transpose(ap(st), ap(R(b3, 256, 384))), [R(b3, 256, 384)], [st])]
+        yield "s", [op("v", 107, lambda e: e.tensor_tensor_scan(ap(pm), ap(R("RST")), ap(st), 0.0, A.mult, A.max), [R("RST"), st], [pm])]
+        yield "s", [tt(u, pm, st, A.is_equal, extra=[co], iap=ap(pm).indirect(ap(co)), ind=True)]
+        o = R(b3, 384, 512)
+        yield "s", [op("v", 54, lambda e: e.transpose(ap(ut), ap(u)), [u], [ut]),
+                    mm(o, R("IHF"), q, True, False), mm(o, R("QC"), one, False, False), mm(o, R("DEB"), ut, False, True)]
+        yc = R(by, 128 * t, 128 * t + 128)
+        yield "s", [ts(R("QS%s%d" % (x, t)), o, BIG, -BIG, A.add, A.add), send(x, t, "QS", "LQ", "aq"),
+                    mm(yc, R("TK", 0, 8), ut, True, True, oap=T[by][0:8, yc[1]:yc[2]])]
+        if t + 1 < STEPS:
+            threads.append([x, main(x, t + 1), None])
+        c = 256 * t + 128 * CH.index(x)
+        yield "k", [op("s", 170, lambda e: e.activation(T.YT[0:8, c:c + 128], T[by][0:8, yc[1]:yc[2]], ActivationFunctionType.Copy, bias=15.0, scale=-1.0),
+                       [yc], [R("YT", c, c + 128)])]
+
+    for x in CH:
+        threads.append([x, keys(x, 0), None])
+        threads.append([x, main(x, 0), None])
+    prog = {"F": 0, "B": 0}
+    while threads:
+        best = None
+        for th in list(threads):
+            if th[2] is None:
+                try:
+                    th[2] = next(th[1])
+                except StopIteration:
+                    threads.remove(th)
+                    continue
+                if th[2] is None:
+                    continue
+            kind, job = th[2]
+            alts = job if isinstance(job, tuple) else (job,)
+            d = min(alts, key=lambda a: start_of(a[0]) + a[0][1] + (PL["v" + kind] if a[0][0] == "v" and kind in "ek" else 0.0))
+            k = start_of(d[0]) + PL[kind] + (PL["lag"] if kind in "xe" and prog[th[0]] < max(prog.values()) else 0.0)
+            if best is None or k < best[0]:
+                best = (k, th, d)
+        if best:
+            best[1][2] = None
+            prog[best[1][0]] += 1
+            for d in best[2]:
+                emit(d)
+
+    for i, x in enumerate(CH):
+        lp = R("LP%s%d" % (x, STEPS))
+        if closing(x):
+            moved(x, lp, False)
+            lp = R("W2" + x)
+        emit(vcopy(R("YP", 128 * i, 128 * i + 128), lp))
+    outs = []
+
+    def out(q, dst, src, reads, sem):
+        emit(op(q, 60, lambda e: e.dma_start(dst, src), reads, [], sem, 16))
+        outs.append(sem)
+    for i, x in enumerate(CH):
+        yp = R("YP", 128 * i, 128 * i + 128)
+        out("y", T.yp[:, 128 * i:128 * i + 128], ap(yp), [yp], "oy" + x)
+    out("y", T.yt[:, :], T.YT[0:8, :], [R("YT")], "oyt")
+    for i, x in enumerate(CH):
+        lq = R("LQ%s%d" % (x, STEPS))
+        out("y", T.yq[:, 128 * i:128 * i + 128], ap(lq), [lq], "oq" + x)
+    for s in outs:
+        g.sync.wait_ge(T.sem[s], 16)
+    for s in ("vs", "ss", "ts", "gs", "lsent"):
+        if know["g"].get(s, 0) < cnt[s]:
+            g.wait_ge(T.sem[s], cnt[s])

@@ -1,14 +1,17 @@
 from concourse.mybir import dt, AluOpType, AxisListType, ActivationFunctionType
 
 A = AluOpType
-CH = ("F", "B")
+L = 64
+NC = 256 // L
+REP = 4
+CK, CE = 32, 32
 STEPS = 4
+PAD = 16
 BIG = 12582912.0
-PL = {"cyc": 0.83, "pe": 0.45, "ga": 1.6, "hop": 110.0, "pipe": 70.0, "rem": 3600.0, "load": 3000.0, "chunk": 32,
-      "s": 0.0, "x": 0.0, "e": 450.0, "k": 600.0, "n": 100.0, "lag": 0.0, "ve": 0.0, "vk": 300.0}
+PLAN = "ejggfiGclalggceeccllcickkhkckecdkeaaalccaaclhhllchacaahdcffamcCaacadfdcaafacddbccdddcabbbdbbaagagddagdbabddbcbDggdeebebccbccbecaddddceabdhbccbaacahabbhccbabacabaccCahfhdacddaddfcacdccfaAbfadcddfbbbgadbbadadagdbbaggedgbbDedcdebcbcbccebbdcadddccbecdcbaaacaabbcbhcbhaaahbcadCacfhfchddaddafdfccaaacdcddcbdfabbgbddbbaadaagbbgbagdcdbDgcdbebbccbeeccdddadeeccabbbdcacaaabbcbbaccbhaacdhhffachCaahdacdddadfccbfadcddfcbbaadcbbbaddadababbddapbbbbbdbBdrdbdddnbbdbbbnsnoooooqoo"
 
 SCRATCH = {}
-SEMAPHORES = ["vs", "ss", "ts", "gs", "lsent", "oyt"]
+SEMAPHORES = ["vs", "ss", "ts", "gs", "lsent", "oyt", "oyp"]
 BF, HF, F32, I32, U16 = "bfloat16", "float16", "float32", "int32", "uint16"
 
 
@@ -17,40 +20,38 @@ def _sb(dtype, cols, names, suffix=""):
         SCRATCH[nm + suffix] = ("sbuf", [128, cols], dtype)
 
 
-_sb(BF, 4096, "s_key s_em")
+_sb(BF, 4096 + 2 * PAD, "s_key s_em")
 _sb(I32, 1024, "s_cl")
 _sb(I32, 256, "s_pl")
 _sb(BF, 256, "s_q")
 _sb(BF, 16, "s_emb s_w BD8 TK")
 _sb(F32, 8, "s_th BDF KC")
 SEMAPHORES += ["l" + k for k in SCRATCH if k[0] == "s"]
-_sb(BF, 128, "ONE IB T1 BD LT VB0 VBT I16 IHF NBD LTM WA WX CA XC QC DEB MASK")
+_sb(BF, 128, "ONE IB NI T1 T2 T3 BD LT VB0 VBT I16 IHF NBD LTM TOT WA WX CA XU XD QC DEB MASK")
 _sb(HF, 128, "IH IH4 BDH")
 _sb(BF, 144, "BM1 B2")
 _sb(F32, 128, "RST")
 _sb(I32, 128, "MI MJ")
 _sb(I32, 8, "COI")
 _sb(U16, 16, "CO")
-_sb(F32, 1024, "CLT YT")
+_sb(F32, 1040, "CLT")
+_sb(F32, 1024, "YT")
 _sb(F32, 256, "YP")
-for _x in CH:
-    _sb(BF, 2048, "K MX E", _x)
-    _sb(U16, 128, "P0 PW", _x)
-    _sb(HF, 128, "PF R NP NQ Z M", _x)
-    _sb(BF, 128, "NE NN U UT", _x)
-    _sb(U16, 16, "COF", _x)
-    _sb(F32, 128, "ST PM SC", _x)
-    _sb(I32, 128, "W1 W2", _x)
-    for _t in range(STEPS):
-        _sb(U16, 128, "PS", "%s%d" % (_x, _t))
-        _sb(BF, 128, "QS", "%s%d" % (_x, _t))
-        _sb(U16, 128, "LP", "%s%d" % (_x, _t + 1))
-        _sb(BF, 128, "LQ", "%s%d" % (_x, _t + 1))
-        SEMAPHORES += ["ap%s%d" % (_x, _t + 1), "aq%s%d" % (_x, _t + 1)]
-    SEMAPHORES += ["oy" + _x, "oq" + _x]
+_sb(I32, 256, "WI WJ")
+_sb(BF, 1024, "UT QS LQ")
+_sb(U16, 1024, "PS PW LP")
+_sb(U16, 256, "P0")
+for _x in range(NC):
+    _s = str(_x)
+    _sb(BF, 16 * L, "K MX E", _s)
+    _sb(HF, L, "R NQ M", _s)
+    _sb(HF, 2 * L, "Z", _s)
+    _sb(BF, L, "NE NN U", _s)
+    _sb(U16, 16, "COF", _s)
+    _sb(F32, L, "ST PM SC", _s)
+    SEMAPHORES += ["%s%d%d" % (a, _x, t) for a in ("ap", "aq") for t in range(STEPS)] + ["oq" + _s]
 for _k in range(8):
     SCRATCH["b%d" % _k] = ("psum", [128, 512], F32)
-SIZE = {BF: 2, HF: 2, U16: 2, F32: 4, I32: 4}
 
 
 def rank_program(g, core, T, topo):
@@ -61,7 +62,6 @@ def rank_program(g, core, T, topo):
     Q = {"v": g.vector, "s": g.scalar, "t": g.tensor, "g": g, "y": g.sync}
     OWN = {"v": "vs", "s": "ss", "t": "ts", "g": "gs"}
     cnt = {"vs": 0, "ss": 0, "ts": 0, "gs": 0, "lsent": 0}
-    clk = {q: 0.0 for q in Q}
     know = {q: {} for q in Q}
     acc = {}
     bank = {}
@@ -69,7 +69,7 @@ def rank_program(g, core, T, topo):
 
     def need(q, toks):
         kn = know[q]
-        for o, sem, val, snap, tm, oq in sorted(toks, key=lambda a: -a[0]):
+        for o, sem, val, snap in sorted(toks, key=lambda a: -a[0]):
             if kn.get(sem, 0) >= val:
                 continue
             Q[q].wait_ge(T.sem[sem], val)
@@ -96,24 +96,11 @@ def rank_program(g, core, T, topo):
                         toks.append(e[4])
         return toks
 
-    def start_of(d):
-        q, dur, fn, reads, writes = d[:5]
-        t0 = clk[q]
-        for k in deps(q, reads, writes):
-            t0 = max(t0, k[4] + (PL["pipe"] if k[5] == q else PL["hop"]))
-        return t0
-
-    def emit(d, quiet=False):
-        q, dur, fn, reads, writes, sem, inc = d
-        t0 = start_of(d)
-        if quiet:
-            t0, dur = max(k[4] for k in deps(q, reads, writes)), 0.0
+    def emit(d):
+        q, fn, reads, writes, sem, inc = d
         need(q, deps(q, reads, writes))
         ins = fn(Q[q])
         seq[0] += 1
-        end = t0 + dur
-        if not quiet:
-            clk[q] = end
         if ins is None:
             return
         if sem is None:
@@ -122,9 +109,8 @@ def rank_program(g, core, T, topo):
             val = cnt[sem]
         else:
             val = inc
-            end += PL["load"]
         ins.then_inc(T.sem[sem], inc)
-        note(q, (seq[0], sem, val, dict(know[q]), end, q), reads, writes)
+        note(q, (seq[0], sem, val, dict(know[q])), reads, writes)
 
     def note(q, tok, reads, writes):
         for regs, wr in ((writes, True), (reads, False)):
@@ -135,12 +121,11 @@ def rank_program(g, core, T, topo):
                     d[q] = (tok if wr else lw, tok)
                     continue
                 l = acc.setdefault(name, [])
-                if wr:
-                    l[:] = [e for e in l if not (lo <= e[0] and e[1] <= hi)]
+                l[:] = [e for e in l if not (lo <= e[0] and e[1] <= hi and (wr or (e[3] == q and not e[2])))]
                 l.append((lo, hi, wr, q, tok))
 
-    def op(q, dur, fn, reads, writes, sem=None, inc=1):
-        return (q, dur, fn, reads, writes, sem, inc)
+    def op(q, fn, reads, writes, sem=None, inc=1):
+        return (q, fn, reads, writes, sem, inc)
 
     def ap(r):
         return T[r[0]][:, r[1]:r[2]]
@@ -148,256 +133,241 @@ def rank_program(g, core, T, topo):
     def R(name, lo=0, hi=None):
         return (name, lo, SCRATCH[name][1][1] if hi is None else hi)
 
-    def vcost(regs, n, two=False):
-        c = 2.0 if two else 0.5 if all(SIZE[SCRATCH[r[0]][2]] == 2 for r in regs) else 1.0
-        return max(64.0, n * c) * PL["cyc"]
-
     def ts(out, in0, s1, s2, op0, op1=None, extra=(), oap=None, iap=None):
         a, b = (ap(out) if oap is None else oap), (ap(in0) if iap is None else iap)
-        dur = vcost((out, in0), out[2] - out[1] if oap is None else 8)
         if op1 is None:
-            return op("v", dur, lambda e: e.tensor_scalar(a, b, s1, None, op0), [in0] + list(extra), [out])
-        return op("v", dur, lambda e: e.tensor_scalar(a, b, s1, s2, op0, op1), [in0] + list(extra), [out])
+            return op("v", lambda e: e.tensor_scalar(a, b, s1, None, op0), [in0] + list(extra), [out])
+        return op("v", lambda e: e.tensor_scalar(a, b, s1, s2, op0, op1), [in0] + list(extra), [out])
 
-    def tt(out, in0, in1, o, extra=(), iap=None, ind=False):
+    def tt(out, in0, in1, o, extra=(), iap=None):
         b = ap(in0) if iap is None else iap
-        m = out[2] - out[1]
-        dur = 50 + m * PL["ga"] * PL["cyc"] if ind else vcost((out, in0, in1), m, in0[0][0] != "b" and in1[0][0] != "b")
-        return op("v", dur, lambda e: e.tensor_tensor(ap(out), b, ap(in1), o), [in0, in1] + list(extra), [out])
+        return op("v", lambda e: e.tensor_tensor(ap(out), b, ap(in1), o), [in0, in1] + list(extra), [out])
 
     def vcopy(out, in_, iap=None):
         b = ap(in_) if iap is None else iap
-        return op("v", vcost((out, in_), out[2] - out[1]), lambda e: e.tensor_copy(ap(out), b), [in_], [out])
+        return op("v", lambda e: e.tensor_copy(ap(out), b), [in_], [out])
 
     def fill(reg, c, fap=None):
         a = ap(reg) if fap is None else fap
-        return op("v", vcost((reg,), reg[2]), lambda e: e.memset(a, c), [], [reg])
+        return op("v", lambda e: e.memset(a, c), [], [reg])
 
     def mm(out, lhs, rhs, start, stop, rap=None, oap=None):
         a, b = (ap(out) if oap is None else oap), (ap(rhs) if rap is None else rap)
-        return op("t", max(64, out[2] - out[1]) * PL["pe"], lambda e: e.matmul(a, ap(lhs), b, start, stop), [lhs, rhs], [out])
+        return op("t", lambda e: e.matmul(a, ap(lhs), b, start, stop), [lhs, rhs], [out])
+
+    def scan(out, d1):
+        r = R("RST", 0, out[2] - out[1])
+        return op("v", lambda e: e.tensor_tensor_scan(ap(out), ap(r), ap(d1), 0.0, A.mult, A.max), [r, d1], [out])
+
+    def turn(out, in_):
+        return op("v", lambda e: e.transpose(ap(out), ap(in_)), [in_], [out])
 
     def sel(base, a):
         return R(base, 15 - a, 15 - a + 128)
 
     for nm in "pl key q w th emb cl em".split():
-        src, d = T[nm][:], "s_" + nm
-        emit(op("y", 60, lambda e: e.dma_start(T[d][:, 0:T[nm].shape[1]], src), [], [R(d)], "l" + d, 16))
+        lo = PAD if nm in ("key", "em") else 0
+        src, d = T[nm][:], R("s_" + nm, lo, lo + T[nm].shape[1])
+        emit(op("y", lambda e: e.dma_start(ap(d), src), [], [d], "ls_" + nm, 16))
 
     def aff(out, in_, pattern, cmp, base, cm):
-        emit(op("g", 400, lambda e: e.affine_select(ap(R(out)), ap(R(in_)), pattern, cmp, 0.0, base, cm), [R(in_)], [R(out)]))
+        emit(op("g", lambda e: e.affine_select(ap(R(out)), ap(R(in_)), pattern, cmp, 0.0, base, cm), [R(in_)], [R(out)]))
     emit(fill(R("ONE"), 1.0))
     aff("T1", "ONE", [[-16, 8], [0, 16]], A.is_ge, 0, 1)
     aff("BD", "T1", [[16, 8], [0, 16]], A.is_ge, 15, -1)
     aff("IB", "ONE", [[-1, 128]], A.is_equal, 0, 1)
-    emit(op("g", 340, lambda e: e.iota(T.VB0[:, :], [[0, 8], [-1, 16]], 15, 0, allow_small_or_imprecise_dtypes=True), [], [R("VB0")]))
-    emit(op("g", 150, lambda e: e.iota(T.COI[:, :], [[16, 8]], 15, 0), [], [R("COI")]))
-    emit(op("g", 340, lambda e: e.iota(T.MI[:, :], [[0, 8], [-1, 16]], 128, 1), [], [R("MI")]))
     aff("LT", "BD", [[1, 128]], A.is_gt, 0, -1)
-    for b in ("BM1", "B2", "WA", "WX"):
+    emit(op("g", lambda e: e.iota(T.MI[:, :], [[0, 8], [-1, 16]], 128, 1), [], [R("MI")]))
+    emit(op("g", lambda e: e.iota(T.VB0[:, :], [[0, 8], [-1, 16]], 15, 0, allow_small_or_imprecise_dtypes=True), [], [R("VB0")]))
+    emit(op("g", lambda e: e.iota(T.COI[:, :], [[16, 8]], 15, 0), [], [R("COI")]))
+    for b in ("BM1", "B2", "WA", "WX", "TOT", "XU", "XD"):
         emit(fill(R(b), 0.0))
-    for d in (fill(R("CA"), -2.0 ** -7, T.CA[0:64, :]), fill(R("XC"), 32.0), fill(R("QC"), -2.0 ** -9), fill(R("RST"), 1.0),
-              fill(R("CA"), 2.0 ** -17, T.CA[64:128, :]), fill(R("XC"), 64.0, T.XC[:, 15:128:16]), fill(R("RST"), 0.0, T.RST[:, 0:128:16])):
+    for r in (R("s_key", 0, PAD), R("s_em", 0, PAD), R("CLT", 0, 8), R("CLT", 1032, 1040)):
+        emit(fill(r, 0.0))
+    for d in (fill(R("CA"), -2.0 ** -7, T.CA[0:64, :]), fill(R("QC"), -2.0 ** -9), fill(R("RST"), 1.0),
+              fill(R("XU"), 16.0, T.XU[:, 15:128:16]), fill(R("XD"), 32.0, T.XD[0:64, 15:128:16]), fill(R("CA"), 2.0 ** -17, T.CA[64:128, :]),
+              fill(R("XU"), 64.0, T.XU[0:64, 0:128:16]), fill(R("XD"), 1.0 / 64, T.XD[64:128, 15:128:16]), fill(R("RST"), 0.0, T.RST[:, 0:128:16]),
+              fill(R("XU"), 30.5 / 64, T.XU[64:128, 0:128:16]), fill(R("XD"), 64.0, T.XD[0:64, 0:128:16]), fill(R("XD"), 29.5 / 64, T.XD[64:128, 0:128:16])):
         emit(d)
     emit(vcopy(R("BD8", 0, 8), R("BD"), T.BD[:, 0:128:16]))
     emit(vcopy(R("BDF"), R("BD"), T.BD[:, 0:128:16]))
     emit(ts(R("NBD"), R("BD"), -1.0, None, A.mult))
     emit(ts(R("BM1"), R("BD8", 0, 8), -1.0, None, A.mult, oap=T.BM1[:, 15:128:16]))
     emit(ts(R("B2"), R("BD8", 0, 8), 2.0, None, A.mult, oap=T.B2[:, 15:128:16]))
-    emit(vcopy(R("BDH"), R("BD")))
-    for i, x in enumerate(CH):
-        emit(vcopy(R("P0" + x), R("s_pl", 128 * i, 128 * i + 128)))
+    emit(ts(R("TOT"), R("BD8", 0, 8), -4096.0, None, A.mult, oap=T.TOT[:, 15:128:16]))
+    emit(ts(R("BDH"), R("BD"), 0.25, None, A.mult))
+    emit(vcopy(R("P0"), R("s_pl")))
     emit(vcopy(R("IH"), R("IB")))
-    emit(ts(R("IH4"), R("IB"), 4096.0, None, A.mult))
+    emit(ts(R("IH4"), R("IB"), -4096.0, None, A.mult))
     emit(ts(R("I16"), R("IB"), 16.0, None, A.mult))
     emit(ts(R("IHF"), R("IB"), 0.5, None, A.mult))
-    emit(vcopy(R("CO", 0, 8), R("COI")))
-    emit(ts(R("VBT"), R("VB0"), 1.0 / 128, None, A.mult))
+    emit(ts(R("NI"), R("IB"), -1.0, None, A.mult))
+    emit(tt(R("T2"), R("IB"), R("LT"), A.subtract))
     emit(ts(R("MJ"), R("MI"), 15, None, A.bitwise_and))
-    emit(ts(R("MASK"), R("MJ"), 0.0, -8192.0, A.not_equal, A.mult))
-    emit(ts(R("LTM"), R("LT"), -4096.0, None, A.mult))
-    emit(op("v", 110, lambda e: e.tensor_reduce(T.KC[:, 0:1], T.LT[:, :], AxisListType.X, A.add), [R("LT")], [R("KC")]))
+    emit(op("v", lambda e: e.tensor_reduce(T.KC[:, 0:1], T.LT[:, :], AxisListType.X, A.add), [R("LT")], [R("KC")]))
+    emit(ts(R("LTM"), R("T2"), 4096.0, None, A.mult))
+    emit(ts(R("T3"), R("MJ"), 0.0, -4096.0, A.not_equal, A.mult))
     emit(ts(R("TK", 0, 8), R("BD8", 0, 8), T.KC[:, 0:1], None, A.mult, extra=[R("KC")]))
-    for q in clk:
-        clk[q] = 0.0
+    emit(ts(R("MASK"), R("T3"), 15872.0, None, A.add))
+    emit(ts(R("VBT"), R("VB0"), 1.0 / 128, None, A.mult))
+    emit(vcopy(R("CO", 0, 8), R("COI")))
 
-    BK = {"F": ("b0", "b1", "b2", "b6"), "B": ("b3", "b4", "b5", "b7")}
-    threads = []
-    state = {"F": -1, "B": -1}
-    once = {}
+    def lanes(name, x, t=0):
+        return R(name, 256 * t + L * x, 256 * t + L * x + L)
 
-    def P(x, t):
-        return R("P0" + x) if t == 0 else R("LP%s%d" % (x, t))
+    def up(x):
+        return x < NC // 2
 
-    def QQ(x, t):
-        i = CH.index(x)
-        return R("s_q", 128 * i, 128 * i + 128) if t == 0 else R("LQ%s%d" % (x, t))
+    over, under = rank < STEPS - 1, rank > n - STEPS
 
-    def closing(x):
-        return 1 if (x == "F" and rank == 0) else -1 if (x == "B" and rank == n - 1) else 0
+    def window(name, x, plain=False):
+        return R(name, PAD if up(x) or plain else 0, 4096 + (2 * PAD if up(x) and over and not plain else PAD))
 
-    def gather(out, win, off, c0, c1):
-        w = R(win)
-        o, f = (out, 16 * c0, 16 * c1), (off[0], c0, c1)
+    def gather(out, w, off, c0, c1):
+        o, f = (out, 16 * c0, 16 * c1), (off[0], off[1] + c0, off[1] + c1)
         src = ap(w).indirect(ap(f))
-        d = 16 * (c1 - c0) * PL["ga"] * PL["cyc"]
-        return ([op("s", 65 + d, lambda e: e.activation(ap(o), src, ActivationFunctionType.Copy), [w, f], [o])],
-                [op("v", 50 + d, lambda e: e.tensor_copy(ap(o), src), [w, f], [o])])
+        return ([op("s", lambda e: e.activation(ap(o), src, ActivationFunctionType.Copy), [w, f], [o])],
+                [op("v", lambda e: e.tensor_copy(ap(o), src), [w, f], [o])])
 
     def send(x, t, src, land, sem):
-        dst = T.cores[(rank + 1) % n if x == "F" else (rank - 1) % n]
-        frm = T.cores[(rank - 1) % n if x == "F" else (rank + 1) % n]
+        dst = T.cores[(rank + 1) % n if up(x) else (rank - 1) % n]
+        frm = T.cores[(rank - 1) % n if up(x) else (rank + 1) % n]
         rid, pid, _ = topo.addr(dst)
-        name = "%s%s%d" % (src, x, t)
-        to, rs = "%s%s%d" % (land, x, t + 1), "%s%s%d" % (sem, x, t + 1)
+        a, to, rs = lanes(src, x, t), lanes(land, x, t), "%s%d%d" % (sem, x, t)
 
         def go(e):
-            t0 = start_of(d)
-            e.remote_dma(T[to][:], T[name][:], T.sem[rs], T.sem.lsent, pid, rid, topo.mask(core, dst))
+            e.remote_dma(ap(to), ap(a), T.sem[rs], T.sem.lsent, pid, rid, topo.mask(core, dst))
             cnt["lsent"] += len(topo.engines(core, dst))
             seq[0] += 1
-            note("r", (seq[0], rs, len(topo.engines(frm, core)), {}, t0 + PL["rem"], "r"), [], [R(to)])
-        d = op("g", 600, go, [R(name)], [])
-        return d
+            note("r", (seq[0], rs, len(topo.engines(frm, core)), {}), [], [to])
+        return op("g", go, [a], [])
 
-    def moved(x, src, quiet):
-        emit(ts(R("W1" + x), src, float(closing(x)), None, A.add), quiet)
-        emit(ts(R("W2" + x), R("W1" + x), 4095, None, A.bitwise_and), quiet)
+    def keys(x):
+        s, bb = str(x), "b%d" % (2 * x + 1)
+        for t in range(STEPS):
+            p = lanes("P0", x) if t == 0 else lanes("LP", x, t - 1)
+            yield [ts(R(bb, L, 2 * L), p, -2048.0 if up(x) else -2047.0 - (PAD if t else 0), None, A.add)]
+            for c in range(0, L, CK):
+                yield gather("K" + s, window("s_key", x, t == 0), p, c, c + CK)
+            for j in range(0, 16, 8):
+                yield [mm(R(bb, 0, L), sel("BM1", i), R("K" + s), i == 0, False, rap=T["K" + s][:, i:16 * L:16]) for i in range(j, j + 8)]
 
-    def keys(x, t):
-        p = src = P(x, t)
-        if closing(x) and t:
-            p = R("PW" + x)
+    def main(x):
+        for t in range(STEPS):
+            for job in step(x, t):
+                yield job
 
-        def first(e):
-            if p != src:
-                moved(x, src, True)
-                emit(vcopy(p, R("W2" + x)), True)
-                need("v", deps("v", [p], []))
-            return e.tensor_scalar(ap(R("PF" + x)), ap(p), -1.0, 8193.5, A.mult, A.add)
-        yield "n", [op("v", vcost((p,), 128), first, [src], [R("PF" + x)])]
-        yield "n", [ts(R(BK[x][0], 128, 256), p, -2048.0, None, A.add)]
-        for c in range(0, 128, PL["chunk"]):
-            yield "k", gather("K" + x, "s_key", p, c, c + PL["chunk"])
-        for j in range(0, 16, 4):
-            yield "n", [mm(R(BK[x][1], 0, 128), sel("BM1", i), R("K" + x), i == 0, False, rap=T["K" + x][:, i:2048:16]) for i in range(j, j + 4)]
-        state[x] = t
-
-    def main(x, t):
-        b1, b2, b3, by = BK[x]
-        q = QQ(x, t)
-        one = R("ONE")
-        while state[x] < t:
-            yield None
-        if "w" not in once:
-            once["w"] = 1
-            for b, c in (("WA", 1.0 / 1024), ("WX", -4.0)):
-                yield "s", [ts(R(b), R("BD8", 0, 8), T.s_w[:, 0:1], c, A.mult, A.mult, extra=[R("s_w")], oap=T[b][:, 15:128:16])]
-        yield "s", [mm(R(b1, 0, 128), R("IB"), q, True, True), mm(R(b2, 0, 128), R("NBD"), q, False, False),
-                    mm(R(b3, 128, 256), R("WA"), q, True, False), mm(R(b3, 128, 256), R("CA"), one, False, True)]
-        for i in range(16):
-            o = R("MX" + x, 128 * i, 128 * i + 128)
-            yield "x", [tt(o, R("K" + x), R(b1, 0, 128), A.max, iap=T["K" + x][:, i:2048:16]), mm(R(b2, 0, 128), sel("B2", i), o, False, i == 15)]
-            if i == 5:
-                l = [ts(R("R" + x), R(b3, 128, 256), BIG, -BIG, A.add, A.add)]
-                for o, last in ((R(b3, 0, 128), True), (R(b3, 128, 256), False)):
-                    l += [mm(o, R("WX"), q, True, False), mm(o, R("XC"), one, False, False), mm(o, R("IH4"), R("R" + x), False, last)]
-                yield "x", l
-            if i == 12:
-                yield "x", [tt(R(b1, 256, 384), R("PF" + x), R(b3, 0, 128), A.subtract)]
-        d, xx, cc = R(b2, 0, 128), R(b3, 128, 256), R(b1, 384, 512)
+    def step(x, t):
+        s, ba, bb = str(x), "b%d" % (2 * x), "b%d" % (2 * x + 1)
+        q = lanes("s_q", x) if t == 0 else lanes("LQ", x, t - 1)
+        one = R("ONE", 0, L)
+        qr, h, xl, xr, pn = R(ba, 0, REP * L), R(ba, 4 * L, 5 * L), R(ba, 5 * L, 6 * L), R(ba, 6 * L, 7 * L), R(ba, 7 * L, 8 * L)
+        d, pm, cc = R(bb, 0, L), R(bb, L, 2 * L), R(bb, 2 * L, 3 * L)
+        yield [mm(qr, R("IB"), q, True, True, oap=T[ba][:, m:REP * L:REP]) for m in range(REP)] + [
+            mm(h, R("WA"), q, True, False), mm(h, R("CA"), one, False, True)]
+        J = 16 // REP
+        for j in range(J):
+            o = R("MX" + s, REP * L * j, REP * L * (j + 1))
+            l = [tt(o, R("K" + s), qr, A.max, iap=T["K" + s][:, j:16 * L:J])]
+            if j == 0:
+                l += [mm(d, R("NBD"), q, False, False)]
+            l += [mm(d, sel("B2", j + J * m), o, False, j == J - 1 and m == REP - 1, rap=T[o[0]][:, o[1] + m:o[2]:REP]) for m in range(REP)]
+            if j == J - 1:
+                l += [mm(xr, R("WX"), q, True, False), mm(xr, R("XU" if up(x) else "XD"), one, False, False), mm(xr, R("IH4"), R("R" + s), False, False)]
+            yield l
+            if j == 0:
+                yield [ts(R("R" + s), h, BIG, -BIG, A.add, A.add)]
         th = T.s_th[:, 0:1]
-        ne, nn = R("NE" + x), R("NN" + x)
-        yield "s", [ts(ne, d, th, None, A.is_lt, extra=[R("s_th")]), mm(xx, R("LTM"), ne, False, False)]
-        yield "s", [tt(R("NP" + x), ne, R(b1, 256, 384), A.mult), mm(xx, R("IH"), R("NP" + x), False, True)]
-        yield "s", [ts(nn, d, th, None, A.is_ge, extra=[R("s_th")])]
-        yield "s", [tt(R("NQ" + x), ne, R(b1, 128, 256), A.mult), mm(cc, R("IB"), R("MASK"), True, False), mm(R(b2, 128, 256), R("IH"), R("NQ" + x), True, False)]
-        if "c" not in once:
-            once["c"] = 1
-            yield "s", [ts(R("CLT"), R("s_cl"), -2048.0, None, A.add)]
-        yield "s", [ts(R("Z" + x), xx, -4096.0, 0.0, A.add, A.max), mm(cc, R("BDH"), R("Z" + x), False, True)]
-        sc = R("SC" + x)
-        yield "s", [op("v", 107, lambda e: e.tensor_tensor_scan(ap(sc), ap(R("RST")), ap(cc), 0.0, A.mult, A.max), [R("RST"), cc], [sc])]
-        yield "s", [ts(R("COF" + x, 0, 8), sc, -0.25, 1024.0, A.mult, A.add, iap=T["SC" + x][:, 15:128:16])]
-        w, f = R("CLT"), R("COF" + x, 0, 8)
-        yield "s", [tt(R("M" + x), w, nn, A.mult, extra=[f], iap=ap(w).indirect(ap(f)), ind=True), mm(R(b2, 128, 256), R("IH"), R("M" + x), False, True)]
-        ps = R("PS%s%d" % (x, t))
-        yield "s", [ts(ps, R(b2, 128, 256), 2048.0, None, A.add), send(x, t, "PS", "LP", "ap")]
-        if t + 1 < STEPS:
-            threads.append([x, keys(x, t + 1), None])
-        for c in range(0, 128, PL["chunk"]):
-            yield "e", gather("E" + x, "s_em", ps, c, c + PL["chunk"])
-        for c0 in (0, 64):
-            o = R(b3, 256 + c0, 320 + c0)
-            yield "s", [mm(o, R("VBT"), R("ONE", 0, 64), True, False)] + [
-                mm(o, R("I16"), ("E" + x, 16 * c0, 16 * c0 + 1024), False, i == 15, rap=T["E" + x][:, 16 * c0 + i:16 * c0 + 1024:16]) for i in range(16)]
-        st, pm, u, ut, co = R("ST" + x), R("PM" + x), R("U" + x), R("UT" + x), R("CO", 0, 8)
-        if "e" not in once:
-            once["e"] = 1
-            for j in range(8):
-                yield "s", [ts(R("DEB", 16 * j, 16 * j + 16), R("s_emb"), T.BDF[:, j:j + 1], 0.5, A.mult, A.mult, extra=[R("BDF")])]
-        yield "s", [op("v", 107, lambda e: e.transpose(ap(st), ap(R(b3, 256, 384))), [R(b3, 256, 384)], [st])]
-        yield "s", [op("v", 107, lambda e: e.tensor_tensor_scan(ap(pm), ap(R("RST")), ap(st), 0.0, A.mult, A.max), [R("RST"), st], [pm])]
-        yield "s", [tt(u, pm, st, A.is_equal, extra=[co], iap=ap(pm).indirect(ap(co)), ind=True)]
-        o = R(b3, 384, 512)
-        yield "s", [op("v", 54, lambda e: e.transpose(ap(ut), ap(u)), [u], [ut]),
-                    mm(o, R("IHF"), q, True, False), mm(o, R("QC"), one, False, False), mm(o, R("DEB"), ut, False, True)]
-        yc = R(by, 128 * t, 128 * t + 128)
-        yield "s", [ts(R("QS%s%d" % (x, t)), o, BIG, -BIG, A.add, A.add), send(x, t, "QS", "LQ", "aq"),
-                    mm(yc, R("TK", 0, 8), ut, True, True, oap=T[by][0:8, yc[1]:yc[2]])]
-        if t + 1 < STEPS:
-            threads.append([x, main(x, t + 1), None])
-        c = 256 * t + 128 * CH.index(x)
-        yield "k", [op("s", 170, lambda e: e.activation(T.YT[0:8, c:c + 128], T[by][0:8, yc[1]:yc[2]], ActivationFunctionType.Copy, bias=15.0, scale=-1.0),
-                       [yc], [R("YT", c, c + 128)])]
+        ne, nn, nq, z = R("NE" + s), R("NN" + s), R("NQ" + s), R("Z" + s)
+        yield [ts(ne, d, th, None, A.is_lt, extra=[R("s_th")]), mm(xr, R("TOT"), ne, False, True), mm(xl, R("LTM"), ne, True, False)]
+        yield [tt(nq, ne, pm, A.mult), mm(xl, R("IH"), nq, False, True)]
+        yield [ts(nn, d, th, None, A.is_ge, extra=[R("s_th")]), mm(cc, R("IB"), R("MASK", 0, L), True, False)]
+        l = [ts(z, R(ba, xl[1], xr[2]), -4096.0, -2048.0, A.add, A.max), mm(cc, R("BDH"), R(z[0], 0, L), False, False),
+             mm(cc, R("BDH"), R(z[0], L, 2 * L), False, True), mm(pn, R("IH"), nq, True, False)]
+        yield l + ([] if up(x) else [mm(pn, R("NI"), ne, False, False)])
+        sc = R("SC" + s)
+        yield [scan(sc, cc)]
+        w, f = R("CLT"), R("COF" + s, 0, L // 16)
+        yield [ts(f, sc, BIG, -BIG, A.add, A.add, iap=T[sc[0]][:, 15:L:16])]
+        yield [tt(R("M" + s), w, nn, A.mult, extra=[f], iap=ap(w).indirect(ap(f))), mm(pn, R("IH"), R("M" + s), False, True)]
+        ps, c = lanes("PS", x, t), 2048.0 + (0 if up(x) else PAD)
+        if rank == (n - 1 if up(x) else 0):
+            yield [ts(ps, pn, c, None, A.add), ts(lanes("PW", x, t), pn, c + (1 if up(x) else -1), None, A.add), send(x, t, "PW", "LP", "ap")]
+        else:
+            yield [ts(ps, pn, c, None, A.add), send(x, t, "PS", "LP", "ap")]
+        for c in range(0, L, CE):
+            yield gather("E" + s, window("s_em", x), ps, c, c + CE)
+        yield [mm(h, R("VBT"), one, True, False)] + [mm(h, R("I16"), R("E" + s), False, i == 15, rap=T["E" + s][:, i:16 * L:16]) for i in range(16)]
+        st, px, u, ut, co = R("ST" + s), R("PM" + s), R("U" + s), lanes("UT", x, t), R("CO", 0, L // 16)
+        yield [turn(st, h), mm(xl, R("IHF"), q, True, False), mm(xl, R("QC"), one, False, False)]
+        yield [scan(px, st)]
+        yield [tt(u, px, st, A.is_equal, extra=[co], iap=ap(px).indirect(ap(co)))]
+        yield [turn(ut, u), mm(xl, R("DEB"), ut, False, True)]
+        yield [ts(lanes("QS", x, t), xl, BIG, -BIG, A.add, A.add), send(x, t, "QS", "LQ", "aq")]
 
-    for x in CH:
-        threads.append([x, keys(x, 0), None])
-        threads.append([x, main(x, 0), None])
-    prog = {"F": 0, "B": 0}
-    while threads:
-        best = None
-        for th in list(threads):
-            if th[2] is None:
-                try:
-                    th[2] = next(th[1])
-                except StopIteration:
-                    threads.remove(th)
-                    continue
-                if th[2] is None:
-                    continue
-            kind, job = th[2]
-            alts = job if isinstance(job, tuple) else (job,)
-            d = min(alts, key=lambda a: start_of(a[0]) + a[0][1] + (PL["v" + kind] if a[0][0] == "v" and kind in "ek" else 0.0))
-            k = start_of(d[0]) + PL[kind] + (PL["lag"] if kind in "xe" and prog[th[0]] < max(prog.values()) else 0.0)
-            if best is None or k < best[0]:
-                best = (k, th, d)
-        if best:
-            best[1][2] = None
-            prog[best[1][0]] += 1
-            for d in best[2]:
-                emit(d)
+    def pad(name):
+        if over:
+            yield [vcopy(R(name, 4096 + PAD, 4096 + 2 * PAD), R(name, PAD, 2 * PAD))]
+        elif under:
+            yield [vcopy(R(name, 0, PAD), R(name, 4096, 4096 + PAD))]
+        else:
+            yield []
 
-    for i, x in enumerate(CH):
-        lp = R("LP%s%d" % (x, STEPS))
-        if closing(x):
-            moved(x, lp, False)
-            lp = R("W2" + x)
-        emit(vcopy(R("YP", 128 * i, 128 * i + 128), lp))
+    def weights():
+        for b, c in (("WA", 1.0 / 1024), ("WX", 4.0)):
+            yield [ts(R(b), R("BD8", 0, 8), T.s_w[:, 0:1], c, A.mult, A.mult, extra=[R("s_w")], oap=T[b][:, 15:128:16])]
+
+    def clusters():
+        for c in range(0, 1024, 256):
+            yield [ts(R("CLT", 8 + c, 264 + c), R("s_cl", c, c + 256), -2048.0, None, A.add)]
+        if over:
+            yield [ts(R("CLT", 1032, 1040), R("s_cl", 0, 8), -2048.0, None, A.add)]
+        elif under:
+            yield [ts(R("CLT", 0, 8), R("s_cl", 1016, 1024), -2048.0, None, A.add)]
+        else:
+            yield []
+
+    def embeddings():
+        for j in range(8):
+            yield [ts(R("DEB", 16 * j, 16 * j + 16), R("s_emb"), T.BDF[:, j:j + 1], 0.5, A.mult, A.mult, extra=[R("BDF")])]
+
     outs = []
 
     def out(q, dst, src, reads, sem):
-        emit(op(q, 60, lambda e: e.dma_start(dst, src), reads, [], sem, 16))
-        outs.append(sem)
-    for i, x in enumerate(CH):
-        yp = R("YP", 128 * i, 128 * i + 128)
-        out("y", T.yp[:, 128 * i:128 * i + 128], ap(yp), [yp], "oy" + x)
-    out("y", T.yt[:, :], T.YT[0:8, :], [R("YT")], "oyt")
-    for i, x in enumerate(CH):
-        lq = R("LQ%s%d" % (x, STEPS))
-        out("y", T.yq[:, 128 * i:128 * i + 128], ap(lq), [lq], "oq" + x)
-    for s in outs:
-        g.sync.wait_ge(T.sem[s], 16)
+        outs.append((q, sem))
+        return op(q, lambda e: e.dma_start(dst, src), reads, [], sem, 16)
+
+    def tokens():
+        for j in range(2):
+            b, y = R("b%d" % (2 * j)), R("YT", 512 * j, 512 * j + 512)
+            yield [mm(b, R("TK", 0, 8), R("UT", y[1], y[2]), True, True, oap=T[b[0]][0:8, :]),
+                   op("s", lambda e: e.activation(T.YT[0:8, y[1]:y[2]], T[b[0]][0:8, :], ActivationFunctionType.Copy, bias=15.0, scale=-1.0), [b], [y])]
+        yield [out("s", T.yt[:, :], T.YT[0:8, :], [R("YT")], "oyt")]
+
+    def pointers():
+        for lo, c, wrap in ((0, 0.0, rank < STEPS), (128, -float(PAD), rank >= n - STEPS)):
+            lp = R("LP", 256 * (STEPS - 1) + lo, 256 * (STEPS - 1) + lo + 128)
+            a, b, y = R("WI", lo, lo + 128), R("WJ", lo, lo + 128), R("YP", lo, lo + 128)
+            yield [ts(a, lp, c + 4096.0, None, A.add) if wrap else ts(y, lp, c, None, A.add)]
+            yield [ts(b, a, 4095, None, A.bitwise_and)] if wrap else []
+            yield [vcopy(y, b)] if wrap else []
+        yield [out("s", T.yp[:, :], T.YP[:, :], [R("YP")], "oyp")]
+
+    def queries(x):
+        lq = lanes("LQ", x, STEPS - 1)
+        yield [out("y", T.yq[:, L * x:L * x + L], ap(lq), [lq], "oq%d" % x)]
+
+    threads = {"i": weights(), "j": pad("s_key"), "k": clusters(), "l": embeddings(), "m": pad("s_em"), "n": tokens(), "o": pointers()}
+    for x in range(NC):
+        threads["abcd"[x]], threads["efgh"[x]], threads["pqrs"[x]] = main(x), keys(x), queries(x)
+    for ch in PLAN:
+        job = next(threads[ch.lower()])
+        if isinstance(job, tuple):
+            job = job[ch.isupper()]
+        for d in job:
+            emit(d)
+    for q, s in outs:
+        Q[q].wait_ge(T.sem[s], 16)
     for s in ("vs", "ss", "ts", "gs", "lsent"):
         if know["g"].get(s, 0) < cnt[s]:
             g.wait_ge(T.sem[s], cnt[s])

@@ -4,11 +4,14 @@ A = AluOpType
 L = 64
 NC = 256 // L
 REP = 4
-CK, CE = 32, 32
+MAXES = ((0, 4), (1, 4), (2, 4), (3, 2), (7, 2))
+CK, CE = (0, 32, 64), ((0, 20, 64),) * 3 + ((0, 32, 64),)
+NS, NV = 8, 16
 STEPS = 4
 PAD = 16
 BIG = 12582912.0
-PLAN = "ejggfiGclalggceeccllcickkhkckecdkeaaalccaaclhhllchacaahdcffamcCaacadfdcaafacddbccdddcabbbdbbaagagddagdbabddbcbDggdeebebccbccbecaddddceabdhbccbaacahabbhccbabacabaccCahfhdacddaddfcacdccfaAbfadcddfbbbgadbbadadagdbbaggedgbbDedcdebcbcbccebbdcadddccbecdcbaaacaabbcbhcbhaaahbcadCacfhfchddaddafdfccaaacdcddcbdfabbgbddbbaadaagbbgbagdcdbDgcdbebbccbeeccdddadeeccabbbdcacaaabbcbbaccbhaacdhhffachCaahdacdddadfccbfadcddfcbbaadcbbbaddadababbddapbbbbbdbBdrdbdddnbbdbbbnsnoooooqoo"
+HUGE = BIG * 4096
+PLAN = "geaehEigeigcleaaaaadgHalgcclacccaakffhhhalacbdadamcfffcbbabacdbcbcljcadcbdClabaldbacelabcbaebddbccbcdceddcdBedgbbageGggbaabcbabaacbaddhdfccaccdadadcfadhhahadfacAacfbccchafcbcbbababaadbacccdbbddddecbcbbdcgeebecbegdadBbdcdbgdaaaadadbbgbaDbaddbafcgafaadfadcdadfcfcdcchAabchhabccbbbacbadcahcbcaheeddbabdddbcbbdCebecdbBbcdddecadcdcdcDcbadadbabgabbaddbdggadggfFcdahaffcfccccabaacahhahbccbdbbcbcahadcbccadbdcddbcbabdbbabcddacdbcddcddcbbaDcddbabnbbdddbdqrdponoooooosn"
 
 SCRATCH = {}
 SEMAPHORES = ["vs", "ss", "ts", "gs", "lsent", "oyt", "oyp"]
@@ -21,20 +24,19 @@ def _sb(dtype, cols, names, suffix=""):
 
 
 _sb(BF, 4096 + 2 * PAD, "s_key s_em")
-_sb(I32, 1024, "s_cl")
+_sb(I32, 1040, "s_cl")
 _sb(I32, 256, "s_pl")
 _sb(BF, 256, "s_q")
 _sb(BF, 16, "s_emb s_w BD8 TK")
 _sb(F32, 8, "s_th BDF KC")
 SEMAPHORES += ["l" + k for k in SCRATCH if k[0] == "s"]
-_sb(BF, 128, "ONE IB NI T1 T2 T3 BD LT VB0 VBT I16 IHF NBD LTM TOT WA WX CA XU XD QC DEB MASK")
-_sb(HF, 128, "IH IH4 BDH")
+_sb(BF, 128, "ONE HALF IB NI T1 T3 BD LT VB0 VBT I16 IHF NBD LTM TOT WA WX CA CB CU CD XU XD YU YD QC DEB MASK")
+_sb(HF, 128, "IH BDH")
 _sb(BF, 144, "BM1 B2")
 _sb(F32, 128, "RST")
 _sb(I32, 128, "MI MJ")
 _sb(I32, 8, "COI")
 _sb(U16, 16, "CO")
-_sb(F32, 1040, "CLT")
 _sb(F32, 1024, "YT")
 _sb(F32, 256, "YP")
 _sb(I32, 256, "WI WJ")
@@ -44,11 +46,11 @@ _sb(U16, 256, "P0")
 for _x in range(NC):
     _s = str(_x)
     _sb(BF, 16 * L, "K MX E", _s)
-    _sb(HF, L, "R NQ M", _s)
+    _sb(HF, L, "PH", _s)
     _sb(HF, 2 * L, "Z", _s)
-    _sb(BF, L, "NE NN U", _s)
+    _sb(BF, L, "NE U", _s)
     _sb(U16, 16, "COF", _s)
-    _sb(F32, L, "ST PM SC", _s)
+    _sb(F32, L, "ST PM SC M N", _s)
     SEMAPHORES += ["%s%d%d" % (a, _x, t) for a in ("ap", "aq") for t in range(STEPS)] + ["oq" + _s]
 for _k in range(8):
     SCRATCH["b%d" % _k] = ("psum", [128, 512], F32)
@@ -166,7 +168,7 @@ def rank_program(g, core, T, topo):
         return R(base, 15 - a, 15 - a + 128)
 
     for nm in "pl key q w th emb cl em".split():
-        lo = PAD if nm in ("key", "em") else 0
+        lo = PAD if nm in ("key", "em") else 8 if nm == "cl" else 0
         src, d = T[nm][:], R("s_" + nm, lo, lo + T[nm].shape[1])
         emit(op("y", lambda e: e.dma_start(ap(d), src), [], [d], "ls_" + nm, 16))
 
@@ -180,32 +182,36 @@ def rank_program(g, core, T, topo):
     emit(op("g", lambda e: e.iota(T.MI[:, :], [[0, 8], [-1, 16]], 128, 1), [], [R("MI")]))
     emit(op("g", lambda e: e.iota(T.VB0[:, :], [[0, 8], [-1, 16]], 15, 0, allow_small_or_imprecise_dtypes=True), [], [R("VB0")]))
     emit(op("g", lambda e: e.iota(T.COI[:, :], [[16, 8]], 15, 0), [], [R("COI")]))
-    for b in ("BM1", "B2", "WA", "WX", "TOT", "XU", "XD"):
+    for b in ("BM1", "B2", "WA", "WX", "TOT", "XU", "XD", "CA", "CB", "CU", "CD"):
         emit(fill(R(b), 0.0))
-    for r in (R("s_key", 0, PAD), R("s_em", 0, PAD), R("CLT", 0, 8), R("CLT", 1032, 1040)):
+    for r in (R("s_key", 0, PAD), R("s_em", 0, PAD), R("HALF", 0, L)):
         emit(fill(r, 0.0))
-    for d in (fill(R("CA"), -2.0 ** -7, T.CA[0:64, :]), fill(R("QC"), -2.0 ** -9), fill(R("RST"), 1.0),
-              fill(R("XU"), 16.0, T.XU[:, 15:128:16]), fill(R("XD"), 32.0, T.XD[0:64, 15:128:16]), fill(R("CA"), 2.0 ** -17, T.CA[64:128, :]),
-              fill(R("XU"), 64.0, T.XU[0:64, 0:128:16]), fill(R("XD"), 1.0 / 64, T.XD[64:128, 15:128:16]), fill(R("RST"), 0.0, T.RST[:, 0:128:16]),
-              fill(R("XU"), 30.5 / 64, T.XU[64:128, 0:128:16]), fill(R("XD"), 64.0, T.XD[0:64, 0:128:16]), fill(R("XD"), 29.5 / 64, T.XD[64:128, 0:128:16])):
+    for r in (R("s_cl", 0, 8), R("s_cl", 1032, 1040)):
+        emit(fill(r, 0))
+    for d in (fill(R("QC"), -2.0 ** -9), fill(R("RST"), 1.0), fill(R("HALF", L, 2 * L), 1.0), fill(R("YU"), -48.0)):
         emit(d)
+    sums = (("XU", 15, 2048.0, -2.0), ("XD", 15, 2048.0, -2.0), ("CA", 15, HUGE / 2, HUGE / 2), ("CB", 15, -HUGE / 2, -HUGE / 2), ("CU", 15, 2048.0, 0.0),
+            ("CD", 15, 2048.0, 1.0), ("YD", None, -6144.0, -1.0), ("XU", 0, 4096.0, 30.5), ("XD", 0, 4096.0, 29.5))
+    for half in (0, 1):
+        for b, c, s0, s1 in sums:
+            if (s0, s1)[half]:
+                emit(fill(R(b), (s0, s1)[half] / 64, T[b][64 * half:64 * half + 64, :] if c is None else T[b][64 * half:64 * half + 64, c:128:16]))
+    emit(fill(R("RST"), 0.0, T.RST[:, 0:128:16]))
     emit(vcopy(R("BD8", 0, 8), R("BD"), T.BD[:, 0:128:16]))
     emit(vcopy(R("BDF"), R("BD"), T.BD[:, 0:128:16]))
     emit(ts(R("NBD"), R("BD"), -1.0, None, A.mult))
     emit(ts(R("BM1"), R("BD8", 0, 8), -1.0, None, A.mult, oap=T.BM1[:, 15:128:16]))
     emit(ts(R("B2"), R("BD8", 0, 8), 2.0, None, A.mult, oap=T.B2[:, 15:128:16]))
-    emit(ts(R("TOT"), R("BD8", 0, 8), -4096.0, None, A.mult, oap=T.TOT[:, 15:128:16]))
+    emit(ts(R("TOT"), R("BD8", 0, 8), 1.0, None, A.mult, oap=T.TOT[:, 15:128:16]))
     emit(ts(R("BDH"), R("BD"), 0.25, None, A.mult))
     emit(vcopy(R("P0"), R("s_pl")))
     emit(vcopy(R("IH"), R("IB")))
-    emit(ts(R("IH4"), R("IB"), -4096.0, None, A.mult))
     emit(ts(R("I16"), R("IB"), 16.0, None, A.mult))
     emit(ts(R("IHF"), R("IB"), 0.5, None, A.mult))
-    emit(ts(R("NI"), R("IB"), -1.0, None, A.mult))
-    emit(tt(R("T2"), R("IB"), R("LT"), A.subtract))
+    emit(ts(R("NI"), R("IB"), -2.0, None, A.mult))
+    emit(tt(R("LTM"), R("LT"), R("IB"), A.subtract))
     emit(ts(R("MJ"), R("MI"), 15, None, A.bitwise_and))
     emit(op("v", lambda e: e.tensor_reduce(T.KC[:, 0:1], T.LT[:, :], AxisListType.X, A.add), [R("LT")], [R("KC")]))
-    emit(ts(R("LTM"), R("T2"), 4096.0, None, A.mult))
     emit(ts(R("T3"), R("MJ"), 0.0, -4096.0, A.not_equal, A.mult))
     emit(ts(R("TK", 0, 8), R("BD8", 0, 8), T.KC[:, 0:1], None, A.mult, extra=[R("KC")]))
     emit(ts(R("MASK"), R("T3"), 15872.0, None, A.add))
@@ -246,11 +252,11 @@ def rank_program(g, core, T, topo):
         s, bb = str(x), "b%d" % (2 * x + 1)
         for t in range(STEPS):
             p = lanes("P0", x) if t == 0 else lanes("LP", x, t - 1)
-            yield [ts(R(bb, L, 2 * L), p, -2048.0 if up(x) else -2047.0 - (PAD if t else 0), None, A.add)]
-            for c in range(0, L, CK):
-                yield gather("K" + s, window("s_key", x, t == 0), p, c, c + CK)
-            for j in range(0, 16, 8):
-                yield [mm(R(bb, 0, L), sel("BM1", i), R("K" + s), i == 0, False, rap=T["K" + s][:, i:16 * L:16]) for i in range(j, j + 8)]
+            yield [ts(R("PH" + s), p, -2048.0 if up(x) else -2047.0 - (PAD if t else 0), None, A.add)]
+            for c0, c1 in zip(CK, CK[1:]):
+                yield gather("K" + s, window("s_key", x, t == 0), p, c0, c1)
+            for j in range(0, 16, NS):
+                yield [mm(R(bb, 0, L), sel("BM1", i), R("K" + s), i == 0, False, rap=T["K" + s][:, i:16 * L:16]) for i in range(j, j + NS)]
 
     def main(x):
         for t in range(STEPS):
@@ -262,42 +268,41 @@ def rank_program(g, core, T, topo):
         q = lanes("s_q", x) if t == 0 else lanes("LQ", x, t - 1)
         one = R("ONE", 0, L)
         qr, h, xl, xr, pn = R(ba, 0, REP * L), R(ba, 4 * L, 5 * L), R(ba, 5 * L, 6 * L), R(ba, 6 * L, 7 * L), R(ba, 7 * L, 8 * L)
-        d, pm, cc = R(bb, 0, L), R(bb, L, 2 * L), R(bb, 2 * L, 3 * L)
-        yield [mm(qr, R("IB"), q, True, True, oap=T[ba][:, m:REP * L:REP]) for m in range(REP)] + [
-            mm(h, R("WA"), q, True, False), mm(h, R("CA"), one, False, True)]
-        J = 16 // REP
-        for j in range(J):
-            o = R("MX" + s, REP * L * j, REP * L * (j + 1))
-            l = [tt(o, R("K" + s), qr, A.max, iap=T["K" + s][:, j:16 * L:J])]
-            if j == 0:
+        d, pm, cc, xx = R(bb, 0, L), R("PH" + s), R(bb, 2 * L, 3 * L), R(ba, 5 * L, 7 * L)
+        yield [mm(qr, R("IB"), q, True, True, oap=T[ba][:, m:REP * L:REP]) for m in range(REP)]
+        c = 0
+        for j, r in MAXES:
+            o, last = R("MX" + s, c, c + r * L), c + r * L == 16 * L
+            a, b = T["K" + s][:, j:16 * L:16 // r], T[ba][:, 0:REP * L:REP // r]
+            l = [op("v", lambda e: e.tensor_tensor(ap(o), a, b, A.max), [R("K" + s), qr], [o])]
+            if c == 0:
                 l += [mm(d, R("NBD"), q, False, False)]
-            l += [mm(d, sel("B2", j + J * m), o, False, j == J - 1 and m == REP - 1, rap=T[o[0]][:, o[1] + m:o[2]:REP]) for m in range(REP)]
-            if j == J - 1:
-                l += [mm(xr, R("WX"), q, True, False), mm(xr, R("XU" if up(x) else "XD"), one, False, False), mm(xr, R("IH4"), R("R" + s), False, False)]
+            l += [mm(d, sel("B2", j + 16 // r * m), o, False, last and m == r - 1, rap=T[o[0]][:, o[1] + m:o[2]:r]) for m in range(r)]
+            c += r * L
+            if last:
+                l += [mm(xx, R("XU" if up(x) else "XD"), R("HALF", 0, 2 * L), True, False), mm(xl, R("IH"), pm, False, False)]
+                l += [mm(xr, R(b), r, False, False) for b, r in (("WA", q), ("CA", one), ("CB", one), ("WX", q), ("CU" if up(x) else "CD", one))]
             yield l
-            if j == 0:
-                yield [ts(R("R" + s), h, BIG, -BIG, A.add, A.add)]
         th = T.s_th[:, 0:1]
-        ne, nn, nq, z = R("NE" + s), R("NN" + s), R("NQ" + s), R("Z" + s)
-        yield [ts(ne, d, th, None, A.is_lt, extra=[R("s_th")]), mm(xr, R("TOT"), ne, False, True), mm(xl, R("LTM"), ne, True, False)]
-        yield [tt(nq, ne, pm, A.mult), mm(xl, R("IH"), nq, False, True)]
-        yield [ts(nn, d, th, None, A.is_ge, extra=[R("s_th")]), mm(cc, R("IB"), R("MASK", 0, L), True, False)]
-        l = [ts(z, R(ba, xl[1], xr[2]), -4096.0, -2048.0, A.add, A.max), mm(cc, R("BDH"), R(z[0], 0, L), False, False),
-             mm(cc, R("BDH"), R(z[0], L, 2 * L), False, True), mm(pn, R("IH"), nq, True, False)]
-        yield l + ([] if up(x) else [mm(pn, R("NI"), ne, False, False)])
-        sc = R("SC" + s)
+        ne, z, sc = R("NE" + s), R("Z" + s), R("SC" + s)
+        yield [ts(ne, d, th, -4096.0, A.is_lt, A.mult, extra=[R("s_th")]), mm(xr, R("TOT"), ne, False, False), mm(xl, R("LTM"), ne, False, True),
+               mm(cc, R("IB"), R("MASK", 0, L), True, False)]
+        yield [ts(z, xx, -4096.0, -2048.0, A.add, A.max), mm(cc, R("BDH"), R(z[0], 0, L), False, False), mm(cc, R("BDH"), R(z[0], L, 2 * L), False, True)]
+        yield [mm(pn, R("IH"), pm, True, False), mm(pn, R("YU" if up(x) else "YD"), one, False, False), mm(pn, R("NI"), ne, False, True)]
         yield [scan(sc, cc)]
-        w, f = R("CLT"), R("COF" + s, 0, L // 16)
+        w, f, m, pv = R("s_cl"), R("COF" + s, 0, L // 16), R("M" + s), R("N" + s)
         yield [ts(f, sc, BIG, -BIG, A.add, A.add, iap=T[sc[0]][:, 15:L:16])]
-        yield [tt(R("M" + s), w, nn, A.mult, extra=[f], iap=ap(w).indirect(ap(f))), mm(pn, R("IH"), R("M" + s), False, True)]
-        ps, c = lanes("PS", x, t), 2048.0 + (0 if up(x) else PAD)
+        yield [tt(m, w, ne, A.add, extra=[f], iap=ap(w).indirect(ap(f)))]
+        yield [tt(pv, m, pn, A.max)]
+        ps, c = lanes("PS", x, t), 0.0 if up(x) else float(PAD)
         if rank == (n - 1 if up(x) else 0):
-            yield [ts(ps, pn, c, None, A.add), ts(lanes("PW", x, t), pn, c + (1 if up(x) else -1), None, A.add), send(x, t, "PW", "LP", "ap")]
+            yield [ts(ps, pv, c, None, A.add), ts(lanes("PW", x, t), pv, c + (1 if up(x) else -1), None, A.add), send(x, t, "PW", "LP", "ap")]
         else:
-            yield [ts(ps, pn, c, None, A.add), send(x, t, "PS", "LP", "ap")]
-        for c in range(0, L, CE):
-            yield gather("E" + s, window("s_em", x), ps, c, c + CE)
-        yield [mm(h, R("VBT"), one, True, False)] + [mm(h, R("I16"), R("E" + s), False, i == 15, rap=T["E" + s][:, i:16 * L:16]) for i in range(16)]
+            yield [ts(ps, pv, c, None, A.add), send(x, t, "PS", "LP", "ap")]
+        for c0, c1 in zip(CE[t], CE[t][1:]):
+            yield gather("E" + s, window("s_em", x), ps, c0, c1)
+        for j in range(0, 16, NV):
+            yield [mm(h, R("VBT"), one, True, False)][j:] + [mm(h, R("I16"), R("E" + s), False, i == 15, rap=T["E" + s][:, i:16 * L:16]) for i in range(j, j + NV)]
         st, px, u, ut, co = R("ST" + s), R("PM" + s), R("U" + s), lanes("UT", x, t), R("CO", 0, L // 16)
         yield [turn(st, h), mm(xl, R("IHF"), q, True, False), mm(xl, R("QC"), one, False, False)]
         yield [scan(px, st)]
@@ -314,16 +319,14 @@ def rank_program(g, core, T, topo):
             yield []
 
     def weights():
-        for b, c in (("WA", 1.0 / 1024), ("WX", 4.0)):
+        for b, c in (("WA", -4.0), ("WX", 4.0)):
             yield [ts(R(b), R("BD8", 0, 8), T.s_w[:, 0:1], c, A.mult, A.mult, extra=[R("s_w")], oap=T[b][:, 15:128:16])]
 
     def clusters():
-        for c in range(0, 1024, 256):
-            yield [ts(R("CLT", 8 + c, 264 + c), R("s_cl", c, c + 256), -2048.0, None, A.add)]
         if over:
-            yield [ts(R("CLT", 1032, 1040), R("s_cl", 0, 8), -2048.0, None, A.add)]
+            yield [vcopy(R("s_cl", 1032, 1040), R("s_cl", 8, 16))]
         elif under:
-            yield [ts(R("CLT", 0, 8), R("s_cl", 1016, 1024), -2048.0, None, A.add)]
+            yield [vcopy(R("s_cl", 0, 8), R("s_cl", 1024, 1032))]
         else:
             yield []
 

@@ -5,16 +5,16 @@ L = 64
 NC = 256 // L
 REP = 4
 MAXES = ((0, 4), (1, 4), (2, 4), (3, 2), (7, 2))
-CK, CE = (0, 32, 64), ((0, 20, 64),) * 3 + ((0, 32, 64),)
+CK, CE = ((0, 32, 64),) + ((0, 64, 64),) * 2 + ((0, 32, 64),), ((0, 26, 64),) * 3 + ((0, 32, 64),)
 NS, NV = 8, 16
 STEPS = 4
 PAD = 16
 BIG = 12582912.0
 HUGE = BIG * 4096
-PLAN = "geaehEigeigcleaaaaadgHalgcclacccaakffhhhalacbdadamcfffcbbabacdbcbcljcadcbdClabaldbacelabcbaebddbccbcdceddcdBedgbbageGggbaabcbabaacbaddhdfccaccdadadcfadhhahadfacAacfbccchafcbcbbababaadbacccdbbddddecbcbbdcgeebecbegdadBbdcdbgdaaaadadbbgbaDbaddbafcgafaadfadcdadfcfcdcchAabchhabccbbbacbadcahcbcaheeddbabdddbcbbdCebecdbBbcdddecadcdcdcDcbadadbabgabbaddbdggadggfFcdahaffcfccccabaacahhahbccbdbbcbcahadcbccadbdcddbcbabdbbabcddacdbcddcddcbbaDcddbabnbbdddbdqrdponoooooosn"
+PLAN = "aeeEteiibeaaaagagGcgfahfgccaacfccjafkbhacbhacabhcbdcamlfcbcAacacddabalhaccbabdcadeebbdcbcdgbeecbbecddBcabdadaaabgdbadbgdgbaDbfdcgadcacacacdfadcadfafdcAdhabfcabcbcbcbahcabcahchabCaecdhbcdbdbdbdcebcdbcebecdBcgbaedbadadadabgdbadbgdgbaDbfdcgadcacacacdfadcadfafdcAdhabfcabcbcbcbahcabcahchabdCahbccddbbddcbdcbcbdceeebbgeedcaBddbagdaadgbadabgdbabgcDddbacaccdacdcadadcfadfafffbcAcacabbbbbchhacabcdachhhbbddddbdbacbcdbacbddddcdcbdbcbdcdDdbcbbbddbddpqornndoooosoon"
 
 SCRATCH = {}
-SEMAPHORES = ["vs", "ss", "ts", "gs", "lsent", "oyt", "oyp"]
+SEMAPHORES = ["vs", "ss", "ts", "gs", "lsent", "oyt", "oyp", "lp1"]
 BF, HF, F32, I32, U16 = "bfloat16", "float16", "float32", "int32", "uint16"
 
 
@@ -27,11 +27,13 @@ _sb(BF, 4096 + 2 * PAD, "s_key s_em")
 _sb(I32, 1040, "s_cl")
 _sb(I32, 256, "s_pl")
 _sb(BF, 256, "s_q")
-_sb(BF, 16, "s_emb s_w BD8 TK")
-_sb(F32, 8, "s_th BDF KC")
+_sb(BF, 16, "s_emb s_w BD8")
+_sb(HF, 16, "TK")
+_sb(F32, 16, "EH")
+_sb(F32, 8, "s_th KC")
 SEMAPHORES += ["l" + k for k in SCRATCH if k[0] == "s"]
-_sb(BF, 128, "ONE HALF IB NI T1 T3 BD LT VB0 VBT I16 IHF NBD LTM TOT WA WX CA CB CU CD XU XD YU YD QC DEB MASK")
-_sb(HF, 128, "IH BDH")
+_sb(BF, 128, "ONE HALF IB NI T1 T3 BD LT VB0 VBT I16 IHF NBD LTM TOT WA WX CA CB XU XD YU YD MASK")
+_sb(HF, 128, "IH BDH DEB")
 _sb(BF, 144, "BM1 B2")
 _sb(F32, 128, "RST")
 _sb(I32, 128, "MI MJ")
@@ -40,15 +42,16 @@ _sb(U16, 16, "CO")
 _sb(F32, 1024, "YT")
 _sb(F32, 256, "YP")
 _sb(I32, 256, "WI WJ")
-_sb(BF, 1024, "UT QS LQ")
+_sb(HF, 1024, "UT")
+_sb(BF, 1024, "QS LQ")
 _sb(U16, 1024, "PS PW LP")
 _sb(U16, 256, "P0")
 for _x in range(NC):
     _s = str(_x)
     _sb(BF, 16 * L, "K MX E", _s)
-    _sb(HF, L, "PH", _s)
+    _sb(HF, L, "PH U", _s)
     _sb(HF, 2 * L, "Z", _s)
-    _sb(BF, L, "NE U", _s)
+    _sb(BF, L, "NE", _s)
     _sb(U16, 16, "COF", _s)
     _sb(F32, L, "ST PM SC M N", _s)
     SEMAPHORES += ["%s%d%d" % (a, _x, t) for a in ("ap", "aq") for t in range(STEPS)] + ["oq" + _s]
@@ -167,7 +170,11 @@ def rank_program(g, core, T, topo):
     def sel(base, a):
         return R(base, 15 - a, 15 - a + 128)
 
-    for nm in "pl key q w th emb cl em".split():
+    for nm in "pl0 key pl1 q w th cl em emb".split():
+        if nm[:2] == "pl":
+            d = R("s_pl", 0, L) if nm == "pl0" else R("s_pl", L, 256)
+            emit(op("y", lambda e: e.dma_start(ap(d), T.pl[:, d[1]:d[2]]), [], [d], "ls_pl" if nm == "pl0" else "lp1", 16))
+            continue
         lo = PAD if nm in ("key", "em") else 8 if nm == "cl" else 0
         src, d = T[nm][:], R("s_" + nm, lo, lo + T[nm].shape[1])
         emit(op("y", lambda e: e.dma_start(ap(d), src), [], [d], "ls_" + nm, 16))
@@ -175,48 +182,53 @@ def rank_program(g, core, T, topo):
     def aff(out, in_, pattern, cmp, base, cm):
         emit(op("g", lambda e: e.affine_select(ap(R(out)), ap(R(in_)), pattern, cmp, 0.0, base, cm), [R(in_)], [R(out)]))
     emit(fill(R("ONE"), 1.0))
+    emit(op("g", lambda e: e.iota(T.MI[:, :], [[0, 8], [-1, 16]], 128, 1), [], [R("MI")]))
     aff("T1", "ONE", [[-16, 8], [0, 16]], A.is_ge, 0, 1)
     aff("BD", "T1", [[16, 8], [0, 16]], A.is_ge, 15, -1)
     aff("IB", "ONE", [[-1, 128]], A.is_equal, 0, 1)
     aff("LT", "BD", [[1, 128]], A.is_gt, 0, -1)
-    emit(op("g", lambda e: e.iota(T.MI[:, :], [[0, 8], [-1, 16]], 128, 1), [], [R("MI")]))
-    emit(op("g", lambda e: e.iota(T.VB0[:, :], [[0, 8], [-1, 16]], 15, 0, allow_small_or_imprecise_dtypes=True), [], [R("VB0")]))
     emit(op("g", lambda e: e.iota(T.COI[:, :], [[16, 8]], 15, 0), [], [R("COI")]))
-    for b in ("BM1", "B2", "WA", "WX", "TOT", "XU", "XD", "CA", "CB", "CU", "CD"):
+    emit(op("g", lambda e: e.iota(T.VB0[:, :], [[0, 8], [-1, 16]], 15, 0, allow_small_or_imprecise_dtypes=True), [], [R("VB0")]))
+    for b in ("BM1", "B2", "WA", "WX", "TOT", "XU", "XD", "CA", "CB", "HALF"):
         emit(fill(R(b), 0.0))
-    for r in (R("s_key", 0, PAD), R("s_em", 0, PAD), R("HALF", 0, L)):
+    for r in (R("s_key", 0, PAD), R("s_em", 0, PAD)):
         emit(fill(r, 0.0))
     for r in (R("s_cl", 0, 8), R("s_cl", 1032, 1040)):
         emit(fill(r, 0))
-    for d in (fill(R("QC"), -2.0 ** -9), fill(R("RST"), 1.0), fill(R("HALF", L, 2 * L), 1.0), fill(R("YU"), -48.0)):
+    for d in (fill(R("RST"), 1.0), fill(R("HALF"), 1.0, T.HALF[0:64, L:2 * L]), fill(R("YU"), -48.0), fill(R("CA"), HUGE / 128, T.CA[:, 15:128:16]),
+              fill(R("YD"), -96.0, T.YD[0:64, :]), fill(R("CB"), -HUGE / 128, T.CB[:, 15:128:16]), fill(R("HALF"), 1.0, T.HALF[64:128, 0:L]),
+              fill(R("YD"), -1.0 / 64, T.YD[64:128, :])):
         emit(d)
-    sums = (("XU", 15, 2048.0, -2.0), ("XD", 15, 2048.0, -2.0), ("CA", 15, HUGE / 2, HUGE / 2), ("CB", 15, -HUGE / 2, -HUGE / 2), ("CU", 15, 2048.0, 0.0),
-            ("CD", 15, 2048.0, 1.0), ("YD", None, -6144.0, -1.0), ("XU", 0, 4096.0, 30.5), ("XD", 0, 4096.0, 29.5))
-    for half in (0, 1):
-        for b, c, s0, s1 in sums:
-            if (s0, s1)[half]:
-                emit(fill(R(b), (s0, s1)[half] / 64, T[b][64 * half:64 * half + 64, :] if c is None else T[b][64 * half:64 * half + 64, c:128:16]))
+    sums = (("XU", 15, 2048.0, -2.0, -2048.0, 0.0), ("XD", 15, 2048.0, -2.0, -2048.0, -1.0), ("XU", 0, 4096.0, 30.5, 0.0, 0.0), ("XD", 0, 4096.0, 29.5, 0.0, 0.0))
+    for j in range(4):
+        for e in sums:
+            if e[2 + j]:
+                emit(fill(R(e[0], e[1] + j, e[1] + j + 1), e[2 + j] / 32, T[e[0]][32 * j:32 * j + 32, e[1]:128:16]))
     emit(fill(R("RST"), 0.0, T.RST[:, 0:128:16]))
-    emit(vcopy(R("BD8", 0, 8), R("BD"), T.BD[:, 0:128:16]))
-    emit(vcopy(R("BDF"), R("BD"), T.BD[:, 0:128:16]))
-    emit(ts(R("NBD"), R("BD"), -1.0, None, A.mult))
-    emit(ts(R("BM1"), R("BD8", 0, 8), -1.0, None, A.mult, oap=T.BM1[:, 15:128:16]))
-    emit(ts(R("B2"), R("BD8", 0, 8), 2.0, None, A.mult, oap=T.B2[:, 15:128:16]))
-    emit(ts(R("TOT"), R("BD8", 0, 8), 1.0, None, A.mult, oap=T.TOT[:, 15:128:16]))
-    emit(ts(R("BDH"), R("BD"), 0.25, None, A.mult))
-    emit(vcopy(R("P0"), R("s_pl")))
-    emit(vcopy(R("IH"), R("IB")))
-    emit(ts(R("I16"), R("IB"), 16.0, None, A.mult))
-    emit(ts(R("IHF"), R("IB"), 0.5, None, A.mult))
-    emit(ts(R("NI"), R("IB"), -2.0, None, A.mult))
-    emit(tt(R("LTM"), R("LT"), R("IB"), A.subtract))
     emit(ts(R("MJ"), R("MI"), 15, None, A.bitwise_and))
+    emit(vcopy(R("P0", 0, L), R("s_pl", 0, L)))
+    emit(ts(R("T3", 0, L), R("MJ", 0, L), 0.0, -4096.0, A.not_equal, A.mult))
+    emit(vcopy(R("CO", 8, 16), R("MJ"), T.MJ[:, 0:128:16]))
+    emit(ts(R("BDH"), R("BD"), 0.25, None, A.mult))
+    emit(vcopy(R("IH"), R("IB")))
     emit(op("v", lambda e: e.tensor_reduce(T.KC[:, 0:1], T.LT[:, :], AxisListType.X, A.add), [R("LT")], [R("KC")]))
-    emit(ts(R("T3"), R("MJ"), 0.0, -4096.0, A.not_equal, A.mult))
-    emit(ts(R("TK", 0, 8), R("BD8", 0, 8), T.KC[:, 0:1], None, A.mult, extra=[R("KC")]))
-    emit(ts(R("MASK"), R("T3"), 15872.0, None, A.add))
-    emit(ts(R("VBT"), R("VB0"), 1.0 / 128, None, A.mult))
+    emit(tt(R("LTM"), R("LT"), R("IB"), A.subtract))
+    for j in (1, 2):
+        emit(ts(R("KC", j + 2, j + 3), R("KC", 0, 1), 0.0, 2047.0 + j, A.is_equal, A.mult))
+    emit(ts(R("TK", 0, 8), R("BD"), T.KC[:, 0:1], None, A.mult, extra=[R("KC", 0, 1)], iap=T.BD[:, 0:128:16]))
     emit(vcopy(R("CO", 0, 8), R("COI")))
+    emit(ts(R("KC", 1, 3), R("KC", 3, 5), -4096.0, None, A.add))
+
+    def scaled(out, in_, c, bias=0.0, oap=None, iap=None):
+        a, b = (ap(out) if oap is None else oap), (ap(in_) if iap is None else iap)
+        emit(op("s", lambda e: e.activation(a, b, ActivationFunctionType.Copy, bias=bias, scale=c), [in_], [out]))
+    for b, c in (("BM1", -1.0), ("B2", 2.0), ("TOT", 1.0)):
+        scaled(R(b), R("BD"), c, oap=T[b][:, 15:128:16], iap=T.BD[:, 0:128:16])
+    scaled(R("BD8", 0, 8), R("BD"), 1.0, iap=T.BD[:, 0:128:16])
+    for b, a, c in (("NBD", "BD", -1.0), ("T1", "BD", 0.5), ("I16", "IB", 16.0), ("IHF", "IB", 0.5), ("NI", "IB", -2.0)):
+        scaled(R(b), R(a), c)
+    scaled(R("MASK", 0, L), R("T3", 0, L), 1.0, 15872.0)
+    scaled(R("VBT"), R("VB0"), 1.0 / 128)
 
     def lanes(name, x, t=0):
         return R(name, 256 * t + L * x, 256 * t + L * x + L)
@@ -235,11 +247,10 @@ def rank_program(g, core, T, topo):
         return ([op("s", lambda e: e.activation(ap(o), src, ActivationFunctionType.Copy), [w, f], [o])],
                 [op("v", lambda e: e.tensor_copy(ap(o), src), [w, f], [o])])
 
-    def send(x, t, src, land, sem):
+    def send(x, a, to, rs):
         dst = T.cores[(rank + 1) % n if up(x) else (rank - 1) % n]
         frm = T.cores[(rank - 1) % n if up(x) else (rank + 1) % n]
         rid, pid, _ = topo.addr(dst)
-        a, to, rs = lanes(src, x, t), lanes(land, x, t), "%s%d%d" % (sem, x, t)
 
         def go(e):
             e.remote_dma(ap(to), ap(a), T.sem[rs], T.sem.lsent, pid, rid, topo.mask(core, dst))
@@ -253,8 +264,8 @@ def rank_program(g, core, T, topo):
         for t in range(STEPS):
             p = lanes("P0", x) if t == 0 else lanes("LP", x, t - 1)
             yield [ts(R("PH" + s), p, -2048.0 if up(x) else -2047.0 - (PAD if t else 0), None, A.add)]
-            for c0, c1 in zip(CK, CK[1:]):
-                yield gather("K" + s, window("s_key", x, t == 0), p, c0, c1)
+            for c0, c1 in zip(CK[t], CK[t][1:]):
+                yield gather("K" + s, window("s_key", x, t == 0), p, c0, c1) if c0 < c1 else []
             for j in range(0, 16, NS):
                 yield [mm(R(bb, 0, L), sel("BM1", i), R("K" + s), i == 0, False, rap=T["K" + s][:, i:16 * L:16]) for i in range(j, j + NS)]
 
@@ -281,13 +292,13 @@ def rank_program(g, core, T, topo):
             c += r * L
             if last:
                 l += [mm(xx, R("XU" if up(x) else "XD"), R("HALF", 0, 2 * L), True, False), mm(xl, R("IH"), pm, False, False)]
-                l += [mm(xr, R(b), r, False, False) for b, r in (("WA", q), ("CA", one), ("CB", one), ("WX", q), ("CU" if up(x) else "CD", one))]
+                l += [mm(xr, R(b), r, False, False) for b, r in (("WA", q), ("CA", one), ("CB", one), ("WX", q))]
             yield l
         th = T.s_th[:, 0:1]
         ne, z, sc = R("NE" + s), R("Z" + s), R("SC" + s)
         yield [ts(ne, d, th, -4096.0, A.is_lt, A.mult, extra=[R("s_th")]), mm(xr, R("TOT"), ne, False, False), mm(xl, R("LTM"), ne, False, True),
                mm(cc, R("IB"), R("MASK", 0, L), True, False)]
-        yield [ts(z, xx, -4096.0, -2048.0, A.add, A.max), mm(cc, R("BDH"), R(z[0], 0, L), False, False), mm(cc, R("BDH"), R(z[0], L, 2 * L), False, True)]
+        yield [ts(z, xx, T.KC[:, 1:2] if up(x) else T.KC[:, 2:3], -2048.0, A.add, A.max, extra=[R("KC")]), mm(cc, R("BDH"), R(z[0], 0, L), False, False), mm(cc, R("BDH"), R(z[0], L, 2 * L), False, True)]
         yield [mm(pn, R("IH"), pm, True, False), mm(pn, R("YU" if up(x) else "YD"), one, False, False), mm(pn, R("NI"), ne, False, True)]
         yield [scan(sc, cc)]
         w, f, m, pv = R("s_cl"), R("COF" + s, 0, L // 16), R("M" + s), R("N" + s)
@@ -296,19 +307,20 @@ def rank_program(g, core, T, topo):
         yield [tt(pv, m, pn, A.max)]
         ps, c = lanes("PS", x, t), 0.0 if up(x) else float(PAD)
         if rank == (n - 1 if up(x) else 0):
-            yield [ts(ps, pv, c, None, A.add), ts(lanes("PW", x, t), pv, c + (1 if up(x) else -1), None, A.add), send(x, t, "PW", "LP", "ap")]
+            yield [ts(ps, pv, c, None, A.add), ts(lanes("PW", x, t), pv, c + (1 if up(x) else -1), None, A.add),
+                   send(x, lanes("PW", x, t), lanes("LP", x, t), "ap%d%d" % (x, t))]
         else:
-            yield [ts(ps, pv, c, None, A.add), send(x, t, "PS", "LP", "ap")]
+            yield [ts(ps, pv, c, None, A.add), send(x, ps, lanes("LP", x, t), "ap%d%d" % (x, t))]
         for c0, c1 in zip(CE[t], CE[t][1:]):
             yield gather("E" + s, window("s_em", x), ps, c0, c1)
         for j in range(0, 16, NV):
             yield [mm(h, R("VBT"), one, True, False)][j:] + [mm(h, R("I16"), R("E" + s), False, i == 15, rap=T["E" + s][:, i:16 * L:16]) for i in range(j, j + NV)]
         st, px, u, ut, co = R("ST" + s), R("PM" + s), R("U" + s), lanes("UT", x, t), R("CO", 0, L // 16)
-        yield [turn(st, h), mm(xl, R("IHF"), q, True, False), mm(xl, R("QC"), one, False, False)]
+        yield [turn(st, h), mm(xl, R("IHF"), q, True, False)]
         yield [scan(px, st)]
         yield [tt(u, px, st, A.is_equal, extra=[co], iap=ap(px).indirect(ap(co)))]
         yield [turn(ut, u), mm(xl, R("DEB"), ut, False, True)]
-        yield [ts(lanes("QS", x, t), xl, BIG, -BIG, A.add, A.add), send(x, t, "QS", "LQ", "aq")]
+        yield [ts(lanes("QS", x, t), xl, BIG, -BIG, A.add, A.add), send(x, lanes("QS", x, t), lanes("LQ", x, t), "aq%d%d" % (x, t))]
 
     def pad(name):
         if over:
@@ -317,6 +329,9 @@ def rank_program(g, core, T, topo):
             yield [vcopy(R(name, 0, PAD), R(name, 4096, 4096 + PAD))]
         else:
             yield []
+
+    def starts():
+        yield [vcopy(R("P0", L, 256), R("s_pl", L, 256))]
 
     def weights():
         for b, c in (("WA", -4.0), ("WX", 4.0)):
@@ -331,8 +346,9 @@ def rank_program(g, core, T, topo):
             yield []
 
     def embeddings():
-        for j in range(8):
-            yield [ts(R("DEB", 16 * j, 16 * j + 16), R("s_emb"), T.BDF[:, j:j + 1], 0.5, A.mult, A.mult, extra=[R("BDF")])]
+        w, f = R("EH"), R("CO", 8, 16)
+        yield [ts(w, R("s_emb"), -0.5, None, A.add)]
+        yield [tt(R("DEB"), w, R("T1"), A.mult, extra=[f], iap=ap(w).indirect(ap(f)))]
 
     outs = []
 
@@ -342,7 +358,7 @@ def rank_program(g, core, T, topo):
 
     def tokens():
         for j in range(2):
-            b, y = R("b%d" % (2 * j)), R("YT", 512 * j, 512 * j + 512)
+            b, y = R("b%d" % (4 * j)), R("YT", 512 * j, 512 * j + 512)
             yield [mm(b, R("TK", 0, 8), R("UT", y[1], y[2]), True, True, oap=T[b[0]][0:8, :]),
                    op("s", lambda e: e.activation(T.YT[0:8, y[1]:y[2]], T[b[0]][0:8, :], ActivationFunctionType.Copy, bias=15.0, scale=-1.0), [b], [y])]
         yield [out("s", T.yt[:, :], T.YT[0:8, :], [R("YT")], "oyt")]
@@ -357,10 +373,10 @@ def rank_program(g, core, T, topo):
         yield [out("s", T.yp[:, :], T.YP[:, :], [R("YP")], "oyp")]
 
     def queries(x):
-        lq = lanes("LQ", x, STEPS - 1)
-        yield [out("y", T.yq[:, L * x:L * x + L], ap(lq), [lq], "oq%d" % x)]
+        y = lanes("LQ", x, STEPS - 1)
+        yield [out("y", T.yq[:, L * x:L * x + L], ap(y), [y], "oq%d" % x)]
 
-    threads = {"i": weights(), "j": pad("s_key"), "k": clusters(), "l": embeddings(), "m": pad("s_em"), "n": tokens(), "o": pointers()}
+    threads = {"t": starts(), "i": weights(), "j": pad("s_key"), "k": clusters(), "l": embeddings(), "m": pad("s_em"), "n": tokens(), "o": pointers()}
     for x in range(NC):
         threads["abcd"[x]], threads["efgh"[x]], threads["pqrs"[x]] = main(x), keys(x), queries(x)
     for ch in PLAN:

from concourse.mybir import dt, AluOpType, AxisListType, ActivationFunctionType

A = AluOpType
L = 64
NC = 256 // L
REP = 4
MAXES = ((0, 4), (1, 4), (2, 4), (3, 2), (7, 2))
CK, CE = ((0, 32, 64),) + ((0, 64, 64),) * 2 + ((0, 32, 64),), ((0, 26, 64),) * 3 + ((0, 32, 64),)
NS, NV = 8, 16
STEPS = 4
PAD = 16
BIG = 12582912.0
HUGE = BIG * 4096
PLAN = "aeeEteiibeaaaagagGcgfahfgccaacfccjafkbhacbhacabhcbdcamlfcbcAacacddabalhaccbabdcadeebbdcbcdgbeecbbecddBcabdadaaabgdbadbgdgbaDbfdcgadcacacacdfadcadfafdcAdhabfcabcbcbcbahcabcahchabCaecdhbcdbdbdbdcebcdbcebecdBcgbaedbadadadabgdbadbgdgbaDbfdcgadcacacacdfadcadfafdcAdhabfcabcbcbcbahcabcahchabdCahbccddbbddcbdcbcbdceeebbgeedcaBddbagdaadgbadabgdbabgcDddbacaccdacdcadadcfadfafffbcAcacabbbbbchhacabcdachhhbbddddbdbacbcdbacbddddcdcbdbcbdcdDdbcbbbddbddpqornndoooosoon"

SCRATCH = {}
SEMAPHORES = ["vs", "ss", "ts", "gs", "lsent", "oyt", "oyp", "lp1"]
BF, HF, F32, I32, U16 = "bfloat16", "float16", "float32", "int32", "uint16"


def _sb(dtype, cols, names, suffix=""):
    for nm in names.split():
        SCRATCH[nm + suffix] = ("sbuf", [128, cols], dtype)


_sb(BF, 4096 + 2 * PAD, "s_key s_em")
_sb(I32, 1040, "s_cl")
_sb(I32, 256, "s_pl")
_sb(BF, 256, "s_q")
_sb(BF, 16, "s_emb s_w BD8")
_sb(HF, 16, "TK")
_sb(F32, 16, "EH")
_sb(F32, 8, "s_th KC")
SEMAPHORES += ["l" + k for k in SCRATCH if k[0] == "s"]
_sb(BF, 128, "ONE HALF IB NI T1 T3 BD LT VB0 VBT I16 IHF NBD LTM TOT WA WX CA CB XU XD YU YD MASK")
_sb(HF, 128, "IH BDH DEB")
_sb(BF, 144, "BM1 B2")
_sb(F32, 128, "RST")
_sb(I32, 128, "MI MJ")
_sb(I32, 8, "COI")
_sb(U16, 16, "CO")
_sb(F32, 1024, "YT")
_sb(F32, 256, "YP")
_sb(I32, 256, "WI WJ")
_sb(HF, 1024, "UT")
_sb(BF, 1024, "QS LQ")
_sb(U16, 1024, "PS PW LP")
_sb(U16, 256, "P0")
for _x in range(NC):
    _s = str(_x)
    _sb(BF, 16 * L, "K MX E", _s)
    _sb(HF, L, "PH U", _s)
    _sb(HF, 2 * L, "Z", _s)
    _sb(BF, L, "NE", _s)
    _sb(U16, 16, "COF", _s)
    _sb(F32, L, "ST PM SC M N", _s)
    SEMAPHORES += ["%s%d%d" % (a, _x, t) for a in ("ap", "aq") for t in range(STEPS)] + ["oq" + _s]
for _k in range(8):
    SCRATCH["b%d" % _k] = ("psum", [128, 512], F32)


def rank_program(g, core, T, topo):
    rank = T.rank_of(core)
    if rank is None:
        return
    n = len(T.cores)
    Q = {"v": g.vector, "s": g.scalar, "t": g.tensor, "g": g, "y": g.sync}
    OWN = {"v": "vs", "s": "ss", "t": "ts", "g": "gs"}
    cnt = {"vs": 0, "ss": 0, "ts": 0, "gs": 0, "lsent": 0}
    know = {q: {} for q in Q}
    acc = {}
    bank = {}
    seq = [0]

    def need(q, toks):
        kn = know[q]
        for o, sem, val, snap in sorted(toks, key=lambda a: -a[0]):
            if kn.get(sem, 0) >= val:
                continue
            Q[q].wait_ge(T.sem[sem], val)
            for s, v in snap.items():
                if kn.get(s, 0) < v:
                    kn[s] = v
            kn[sem] = val

    def deps(q, reads, writes):
        toks = []
        for regs, wr in ((reads, False), (writes, True)):
            for name, lo, hi in regs:
                if name[0] == "b":
                    for oq, (lw, la) in bank.get(name, {}).items():
                        if oq != q:
                            toks.append(la)
                        elif q != "t" and not wr and lw is not None:
                            toks.append(lw)
                    continue
                for e in acc.get(name, []):
                    if e[0] < hi and lo < e[1] and (e[2] or wr):
                        if e[3] == q and not e[2]:
                            continue
                        toks.append(e[4])
        return toks

    def emit(d):
        q, fn, reads, writes, sem, inc = d
        need(q, deps(q, reads, writes))
        ins = fn(Q[q])
        seq[0] += 1
        if ins is None:
            return
        if sem is None:
            sem = OWN[q]
            cnt[sem] += 1
            val = cnt[sem]
        else:
            val = inc
        ins.then_inc(T.sem[sem], inc)
        note(q, (seq[0], sem, val, dict(know[q])), reads, writes)

    def note(q, tok, reads, writes):
        for regs, wr in ((writes, True), (reads, False)):
            for name, lo, hi in regs:
                if name[0] == "b":
                    d = bank.setdefault(name, {})
                    lw = d[q][0] if q in d else None
                    d[q] = (tok if wr else lw, tok)
                    continue
                l = acc.setdefault(name, [])
                l[:] = [e for e in l if not (lo <= e[0] and e[1] <= hi and (wr or (e[3] == q and not e[2])))]
                l.append((lo, hi, wr, q, tok))

    def op(q, fn, reads, writes, sem=None, inc=1):
        return (q, fn, reads, writes, sem, inc)

    def ap(r):
        return T[r[0]][:, r[1]:r[2]]

    def R(name, lo=0, hi=None):
        return (name, lo, SCRATCH[name][1][1] if hi is None else hi)

    def ts(out, in0, s1, s2, op0, op1=None, extra=(), oap=None, iap=None):
        a, b = (ap(out) if oap is None else oap), (ap(in0) if iap is None else iap)
        if op1 is None:
            return op("v", lambda e: e.tensor_scalar(a, b, s1, None, op0), [in0] + list(extra), [out])
        return op("v", lambda e: e.tensor_scalar(a, b, s1, s2, op0, op1), [in0] + list(extra), [out])

    def tt(out, in0, in1, o, extra=(), iap=None):
        b = ap(in0) if iap is None else iap
        return op("v", lambda e: e.tensor_tensor(ap(out), b, ap(in1), o), [in0, in1] + list(extra), [out])

    def vcopy(out, in_, iap=None):
        b = ap(in_) if iap is None else iap
        return op("v", lambda e: e.tensor_copy(ap(out), b), [in_], [out])

    def fill(reg, c, fap=None):
        a = ap(reg) if fap is None else fap
        return op("v", lambda e: e.memset(a, c), [], [reg])

    def mm(out, lhs, rhs, start, stop, rap=None, oap=None):
        a, b = (ap(out) if oap is None else oap), (ap(rhs) if rap is None else rap)
        return op("t", lambda e: e.matmul(a, ap(lhs), b, start, stop), [lhs, rhs], [out])

    def scan(out, d1):
        r = R("RST", 0, out[2] - out[1])
        return op("v", lambda e: e.tensor_tensor_scan(ap(out), ap(r), ap(d1), 0.0, A.mult, A.max), [r, d1], [out])

    def turn(out, in_):
        return op("v", lambda e: e.transpose(ap(out), ap(in_)), [in_], [out])

    def sel(base, a):
        return R(base, 15 - a, 15 - a + 128)

    for nm in "pl0 key pl1 q w th cl em emb".split():
        if nm[:2] == "pl":
            d = R("s_pl", 0, L) if nm == "pl0" else R("s_pl", L, 256)
            emit(op("y", lambda e: e.dma_start(ap(d), T.pl[:, d[1]:d[2]]), [], [d], "ls_pl" if nm == "pl0" else "lp1", 16))
            continue
        lo = PAD if nm in ("key", "em") else 8 if nm == "cl" else 0
        src, d = T[nm][:], R("s_" + nm, lo, lo + T[nm].shape[1])
        emit(op("y", lambda e: e.dma_start(ap(d), src), [], [d], "ls_" + nm, 16))

    def aff(out, in_, pattern, cmp, base, cm):
        emit(op("g", lambda e: e.affine_select(ap(R(out)), ap(R(in_)), pattern, cmp, 0.0, base, cm), [R(in_)], [R(out)]))
    emit(fill(R("ONE"), 1.0))
    emit(op("g", lambda e: e.iota(T.MI[:, :], [[0, 8], [-1, 16]], 128, 1), [], [R("MI")]))
    aff("T1", "ONE", [[-16, 8], [0, 16]], A.is_ge, 0, 1)
    aff("BD", "T1", [[16, 8], [0, 16]], A.is_ge, 15, -1)
    aff("IB", "ONE", [[-1, 128]], A.is_equal, 0, 1)
    aff("LT", "BD", [[1, 128]], A.is_gt, 0, -1)
    emit(op("g", lambda e: e.iota(T.COI[:, :], [[16, 8]], 15, 0), [], [R("COI")]))
    emit(op("g", lambda e: e.iota(T.VB0[:, :], [[0, 8], [-1, 16]], 15, 0, allow_small_or_imprecise_dtypes=True), [], [R("VB0")]))
    for b in ("BM1", "B2", "WA", "WX", "TOT", "XU", "XD", "CA", "CB", "HALF"):
        emit(fill(R(b), 0.0))
    for r in (R("s_key", 0, PAD), R("s_em", 0, PAD)):
        emit(fill(r, 0.0))
    for r in (R("s_cl", 0, 8), R("s_cl", 1032, 1040)):
        emit(fill(r, 0))
    for d in (fill(R("RST"), 1.0), fill(R("HALF"), 1.0, T.HALF[0:64, L:2 * L]), fill(R("YU"), -48.0), fill(R("CA"), HUGE / 128, T.CA[:, 15:128:16]),
              fill(R("YD"), -96.0, T.YD[0:64, :]), fill(R("CB"), -HUGE / 128, T.CB[:, 15:128:16]), fill(R("HALF"), 1.0, T.HALF[64:128, 0:L]),
              fill(R("YD"), -1.0 / 64, T.YD[64:128, :])):
        emit(d)
    sums = (("XU", 15, 2048.0, -2.0, -2048.0, 0.0), ("XD", 15, 2048.0, -2.0, -2048.0, -1.0), ("XU", 0, 4096.0, 30.5, 0.0, 0.0), ("XD", 0, 4096.0, 29.5, 0.0, 0.0))
    for j in range(4):
        for e in sums:
            if e[2 + j]:
                emit(fill(R(e[0], e[1] + j, e[1] + j + 1), e[2 + j] / 32, T[e[0]][32 * j:32 * j + 32, e[1]:128:16]))
    emit(fill(R("RST"), 0.0, T.RST[:, 0:128:16]))
    emit(ts(R("MJ"), R("MI"), 15, None, A.bitwise_and))
    emit(vcopy(R("P0", 0, L), R("s_pl", 0, L)))
    emit(ts(R("T3", 0, L), R("MJ", 0, L), 0.0, -4096.0, A.not_equal, A.mult))
    emit(vcopy(R("CO", 8, 16), R("MJ"), T.MJ[:, 0:128:16]))
    emit(ts(R("BDH"), R("BD"), 0.25, None, A.mult))
    emit(vcopy(R("IH"), R("IB")))
    emit(op("v", lambda e: e.tensor_reduce(T.KC[:, 0:1], T.LT[:, :], AxisListType.X, A.add), [R("LT")], [R("KC")]))
    emit(tt(R("LTM"), R("LT"), R("IB"), A.subtract))
    for j in (1, 2):
        emit(ts(R("KC", j + 2, j + 3), R("KC", 0, 1), 0.0, 2047.0 + j, A.is_equal, A.mult))
    emit(ts(R("TK", 0, 8), R("BD"), T.KC[:, 0:1], None, A.mult, extra=[R("KC", 0, 1)], iap=T.BD[:, 0:128:16]))
    emit(vcopy(R("CO", 0, 8), R("COI")))
    emit(ts(R("KC", 1, 3), R("KC", 3, 5), -4096.0, None, A.add))

    def scaled(out, in_, c, bias=0.0, oap=None, iap=None):
        a, b = (ap(out) if oap is None else oap), (ap(in_) if iap is None else iap)
        emit(op("s", lambda e: e.activation(a, b, ActivationFunctionType.Copy, bias=bias, scale=c), [in_], [out]))
    for b, c in (("BM1", -1.0), ("B2", 2.0), ("TOT", 1.0)):
        scaled(R(b), R("BD"), c, oap=T[b][:, 15:128:16], iap=T.BD[:, 0:128:16])
    scaled(R("BD8", 0, 8), R("BD"), 1.0, iap=T.BD[:, 0:128:16])
    for b, a, c in (("NBD", "BD", -1.0), ("T1", "BD", 0.5), ("I16", "IB", 16.0), ("IHF", "IB", 0.5), ("NI", "IB", -2.0)):
        scaled(R(b), R(a), c)
    scaled(R("MASK", 0, L), R("T3", 0, L), 1.0, 15872.0)
    scaled(R("VBT"), R("VB0"), 1.0 / 128)

    def lanes(name, x, t=0):
        return R(name, 256 * t + L * x, 256 * t + L * x + L)

    def up(x):
        return x < NC // 2

    over, under = rank < STEPS - 1, rank > n - STEPS

    def window(name, x, plain=False):
        return R(name, PAD if up(x) or plain else 0, 4096 + (2 * PAD if up(x) and over and not plain else PAD))

    def gather(out, w, off, c0, c1):
        o, f = (out, 16 * c0, 16 * c1), (off[0], off[1] + c0, off[1] + c1)
        src = ap(w).indirect(ap(f))
        return ([op("s", lambda e: e.activation(ap(o), src, ActivationFunctionType.Copy), [w, f], [o])],
                [op("v", lambda e: e.tensor_copy(ap(o), src), [w, f], [o])])

    def send(x, a, to, rs):
        dst = T.cores[(rank + 1) % n if up(x) else (rank - 1) % n]
        frm = T.cores[(rank - 1) % n if up(x) else (rank + 1) % n]
        rid, pid, _ = topo.addr(dst)

        def go(e):
            e.remote_dma(ap(to), ap(a), T.sem[rs], T.sem.lsent, pid, rid, topo.mask(core, dst))
            cnt["lsent"] += len(topo.engines(core, dst))
            seq[0] += 1
            note("r", (seq[0], rs, len(topo.engines(frm, core)), {}), [], [to])
        return op("g", go, [a], [])

    def keys(x):
        s, bb = str(x), "b%d" % (2 * x + 1)
        for t in range(STEPS):
            p = lanes("P0", x) if t == 0 else lanes("LP", x, t - 1)
            yield [ts(R("PH" + s), p, -2048.0 if up(x) else -2047.0 - (PAD if t else 0), None, A.add)]
            for c0, c1 in zip(CK[t], CK[t][1:]):
                yield gather("K" + s, window("s_key", x, t == 0), p, c0, c1) if c0 < c1 else []
            for j in range(0, 16, NS):
                yield [mm(R(bb, 0, L), sel("BM1", i), R("K" + s), i == 0, False, rap=T["K" + s][:, i:16 * L:16]) for i in range(j, j + NS)]

    def main(x):
        for t in range(STEPS):
            for job in step(x, t):
                yield job

    def step(x, t):
        s, ba, bb = str(x), "b%d" % (2 * x), "b%d" % (2 * x + 1)
        q = lanes("s_q", x) if t == 0 else lanes("LQ", x, t - 1)
        one = R("ONE", 0, L)
        qr, h, xl, xr, pn = R(ba, 0, REP * L), R(ba, 4 * L, 5 * L), R(ba, 5 * L, 6 * L), R(ba, 6 * L, 7 * L), R(ba, 7 * L, 8 * L)
        d, pm, cc, xx = R(bb, 0, L), R("PH" + s), R(bb, 2 * L, 3 * L), R(ba, 5 * L, 7 * L)
        yield [mm(qr, R("IB"), q, True, True, oap=T[ba][:, m:REP * L:REP]) for m in range(REP)]
        c = 0
        for j, r in MAXES:
            o, last = R("MX" + s, c, c + r * L), c + r * L == 16 * L
            a, b = T["K" + s][:, j:16 * L:16 // r], T[ba][:, 0:REP * L:REP // r]
            l = [op("v", lambda e: e.tensor_tensor(ap(o), a, b, A.max), [R("K" + s), qr], [o])]
            if c == 0:
                l += [mm(d, R("NBD"), q, False, False)]
            l += [mm(d, sel("B2", j + 16 // r * m), o, False, last and m == r - 1, rap=T[o[0]][:, o[1] + m:o[2]:r]) for m in range(r)]
            c += r * L
            if last:
                l += [mm(xx, R("XU" if up(x) else "XD"), R("HALF", 0, 2 * L), True, False), mm(xl, R("IH"), pm, False, False)]
                l += [mm(xr, R(b), r, False, False) for b, r in (("WA", q), ("CA", one), ("CB", one), ("WX", q))]
            yield l
        th = T.s_th[:, 0:1]
        ne, z, sc = R("NE" + s), R("Z" + s), R("SC" + s)
        yield [ts(ne, d, th, -4096.0, A.is_lt, A.mult, extra=[R("s_th")]), mm(xr, R("TOT"), ne, False, False), mm(xl, R("LTM"), ne, False, True),
               mm(cc, R("IB"), R("MASK", 0, L), True, False)]
        yield [ts(z, xx, T.KC[:, 1:2] if up(x) else T.KC[:, 2:3], -2048.0, A.add, A.max, extra=[R("KC")]), mm(cc, R("BDH"), R(z[0], 0, L), False, False), mm(cc, R("BDH"), R(z[0], L, 2 * L), False, True)]
        yield [mm(pn, R("IH"), pm, True, False), mm(pn, R("YU" if up(x) else "YD"), one, False, False), mm(pn, R("NI"), ne, False, True)]
        yield [scan(sc, cc)]
        w, f, m, pv = R("s_cl"), R("COF" + s, 0, L // 16), R("M" + s), R("N" + s)
        yield [ts(f, sc, BIG, -BIG, A.add, A.add, iap=T[sc[0]][:, 15:L:16])]
        yield [tt(m, w, ne, A.add, extra=[f], iap=ap(w).indirect(ap(f)))]
        yield [tt(pv, m, pn, A.max)]
        ps, c = lanes("PS", x, t), 0.0 if up(x) else float(PAD)
        if rank == (n - 1 if up(x) else 0):
            yield [ts(ps, pv, c, None, A.add), ts(lanes("PW", x, t), pv, c + (1 if up(x) else -1), None, A.add),
                   send(x, lanes("PW", x, t), lanes("LP", x, t), "ap%d%d" % (x, t))]
        else:
            yield [ts(ps, pv, c, None, A.add), send(x, ps, lanes("LP", x, t), "ap%d%d" % (x, t))]
        for c0, c1 in zip(CE[t], CE[t][1:]):
            yield gather("E" + s, window("s_em", x), ps, c0, c1)
        for j in range(0, 16, NV):
            yield [mm(h, R("VBT"), one, True, False)][j:] + [mm(h, R("I16"), R("E" + s), False, i == 15, rap=T["E" + s][:, i:16 * L:16]) for i in range(j, j + NV)]
        st, px, u, ut, co = R("ST" + s), R("PM" + s), R("U" + s), lanes("UT", x, t), R("CO", 0, L // 16)
        yield [turn(st, h), mm(xl, R("IHF"), q, True, False)]
        yield [scan(px, st)]
        yield [tt(u, px, st, A.is_equal, extra=[co], iap=ap(px).indirect(ap(co)))]
        yield [turn(ut, u), mm(xl, R("DEB"), ut, False, True)]
        yield [ts(lanes("QS", x, t), xl, BIG, -BIG, A.add, A.add), send(x, lanes("QS", x, t), lanes("LQ", x, t), "aq%d%d" % (x, t))]

    def pad(name):
        if over:
            yield [vcopy(R(name, 4096 + PAD, 4096 + 2 * PAD), R(name, PAD, 2 * PAD))]
        elif under:
            yield [vcopy(R(name, 0, PAD), R(name, 4096, 4096 + PAD))]
        else:
            yield []

    def starts():
        yield [vcopy(R("P0", L, 256), R("s_pl", L, 256))]

    def weights():
        for b, c in (("WA", -4.0), ("WX", 4.0)):
            yield [ts(R(b), R("BD8", 0, 8), T.s_w[:, 0:1], c, A.mult, A.mult, extra=[R("s_w")], oap=T[b][:, 15:128:16])]

    def clusters():
        if over:
            yield [vcopy(R("s_cl", 1032, 1040), R("s_cl", 8, 16))]
        elif under:
            yield [vcopy(R("s_cl", 0, 8), R("s_cl", 1024, 1032))]
        else:
            yield []

    def embeddings():
        w, f = R("EH"), R("CO", 8, 16)
        yield [ts(w, R("s_emb"), -0.5, None, A.add)]
        yield [tt(R("DEB"), w, R("T1"), A.mult, extra=[f], iap=ap(w).indirect(ap(f)))]

    outs = []

    def out(q, dst, src, reads, sem):
        outs.append((q, sem))
        return op(q, lambda e: e.dma_start(dst, src), reads, [], sem, 16)

    def tokens():
        for j in range(2):
            b, y = R("b%d" % (4 * j)), R("YT", 512 * j, 512 * j + 512)
            yield [mm(b, R("TK", 0, 8), R("UT", y[1], y[2]), True, True, oap=T[b[0]][0:8, :]),
                   op("s", lambda e: e.activation(T.YT[0:8, y[1]:y[2]], T[b[0]][0:8, :], ActivationFunctionType.Copy, bias=15.0, scale=-1.0), [b], [y])]
        yield [out("s", T.yt[:, :], T.YT[0:8, :], [R("YT")], "oyt")]

    def pointers():
        for lo, c, wrap in ((0, 0.0, rank < STEPS), (128, -float(PAD), rank >= n - STEPS)):
            lp = R("LP", 256 * (STEPS - 1) + lo, 256 * (STEPS - 1) + lo + 128)
            a, b, y = R("WI", lo, lo + 128), R("WJ", lo, lo + 128), R("YP", lo, lo + 128)
            yield [ts(a, lp, c + 4096.0, None, A.add) if wrap else ts(y, lp, c, None, A.add)]
            yield [ts(b, a, 4095, None, A.bitwise_and)] if wrap else []
            yield [vcopy(y, b)] if wrap else []
        yield [out("s", T.yp[:, :], T.YP[:, :], [R("YP")], "oyp")]

    def queries(x):
        y = lanes("LQ", x, STEPS - 1)
        yield [out("y", T.yq[:, L * x:L * x + L], ap(y), [y], "oq%d" % x)]

    threads = {"t": starts(), "i": weights(), "j": pad("s_key"), "k": clusters(), "l": embeddings(), "m": pad("s_em"), "n": tokens(), "o": pointers()}
    for x in range(NC):
        threads["abcd"[x]], threads["efgh"[x]], threads["pqrs"[x]] = main(x), keys(x), queries(x)
    for ch in PLAN:
        job = next(threads[ch.lower()])
        if isinstance(job, tuple):
            job = job[ch.isupper()]
        for d in job:
            emit(d)
    for q, s in outs:
        Q[q].wait_ge(T.sem[s], 16)
    for s in ("vs", "ss", "ts", "gs", "lsent"):
        if know["g"].get(s, 0) < cnt[s]:
            g.wait_ge(T.sem[s], cnt[s])
